import numpy as np, ml_dtypes
CORES = [3,11,19,27,35,43,51,59]
N = 8
BF = ml_dtypes.bfloat16
def gentries(a):
    return np.ascontiguousarray(a.reshape(8, 16, -1).transpose(0, 2, 1)).reshape(8, -1)
def gtable(e):
    e = np.asarray(e); return np.ascontiguousarray(e.reshape(8, -1, 16).transpose(0, 2, 1)).reshape(128, -1).astype(np.int32)
W, n, V, C, Z = 4, 4096, 16384, 1024, 256
def counts(rng, h, z):
    c = np.zeros((N, 8, W), np.int64)
    for r in range(N):
        for g in range(8):
            m = int(h[r, g] - z[r, g]) - (W - 2); b = np.sort(rng.integers(0, m + 1, W - 3))
            c[r, g, 0] = n - h[r, g]; c[r, g, 1:W - 1] = np.diff(np.concatenate([[0], b, [m]])) + 1; c[r, g, W - 1] = z[r, g]
    return c
def some(rng):
    return rng.integers(C - C // 4, C + 1, (N, 8)), rng.integers(Z // 2, Z + 1, (N, 8))
def names(rng):
    return np.stack([np.stack([rng.permutation(V)[:n] for g in range(8)]) for r in range(N)]).astype(np.int64)
def depths(rng, c):
    return np.stack([np.stack([rng.permutation(np.repeat(np.arange(W), c[r, g])) for g in range(8)]) for r in range(N)])
def link(rng, o, dep):
    x = np.zeros((N, 8, n), np.int64)
    for r in range(N):
        q = (r + 1) % N
        for g in range(8):
            m = np.ones(V, bool); m[o[q, g]] = False; free = np.flatnonzero(m)
            v = free[rng.integers(0, len(free), n)]
            for k in range(1, W):
                i = np.flatnonzero(dep[r, g] == k)
                if len(i):
                    t = np.flatnonzero(dep[q, g] == k - 1 if k < W - 1 else dep[q, g] >= W - 2)
                    v[i] = o[q, g][t[rng.integers(0, len(t), len(i))]]
            x[r, g] = v
    return x
def pack(o, x, s):
    return {"own": np.stack([gtable(a) for a in o]), "nxt": np.stack([gtable(a) for a in x]), "pts": np.asarray(s).astype(np.int32)}
def points(rng):
    return rng.integers(0, 256, (N, 8, n))
def setup_inputs(rng):
    h, z = some(rng); o = names(rng); dep = depths(rng, counts(rng, h, z))
    return pack(o, link(rng, o, dep), points(rng))
def setup_inputs_full(rng):
    o = names(rng); c = counts(rng, np.full((N, 8), C), np.full((N, 8), Z)); e = rng.permutation(8)[:4]
    c[:, e, 1:W - 2] = 1; c[:, e, W - 2] = C - Z - (W - 3)
    dep = depths(rng, c)
    return pack(o, link(rng, o, dep), points(rng))
def setup_inputs_few(rng):
    h, z = some(rng); e = rng.permutation(8); q = int(rng.integers(0, N)); o = names(rng)
    z[:, e[2]] = 1; z[:, e[3]] = np.where(rng.random(N) < 0.5, 0, z[:, e[3]]); z[q, e[3]] = 0; z[:, e[4]] = Z; h[:, e[4]] = C
    c = counts(rng, h, z); c[:, e[0], 0] = n; c[:, e[0], 1:] = 0
    for t in range(W - 1):
        r = (q - t) % N; c[r, e[1], 0] += np.sum(c[r, e[1], t + 1:]); c[r, e[1], t + 1:] = 0
    dep = depths(rng, c)
    return pack(o, link(rng, o, dep), points(rng))
def setup_inputs_repeats(rng):
    h, z = some(rng); o = names(rng); dep = depths(rng, counts(rng, h, z)); x = link(rng, o, dep)
    for r in range(N):
        for g in range(8):
            for k in (0, W - 1):
                i = np.flatnonzero(dep[r, g] == k); x[r, g, i] = x[r, g, i[0]]
    return pack(o, x, points(rng))
def setup_inputs_ends(rng):
    h, z = some(rng); dep = depths(rng, counts(rng, h, z))
    o = 1 + np.stack([np.stack([rng.permutation(V - 2)[:n] for g in range(8)]) for r in range(N)]).astype(np.int64)
    for r in range(N):
        for g in range(0, 8, 2):
            o[r, g, 0] = 0; o[r, g, n - 1] = V - 1; a = dep[r, g]
            i = np.flatnonzero(a == W - 1); j = i[rng.integers(0, len(i))]; u, v = int(a[0]), int(a[j]); a[j] = u; a[0] = v
            i = np.flatnonzero(a[1:] == W - 1) + 1; j = i[rng.integers(0, len(i))]; u, v = int(a[n - 1]), int(a[j]); a[j] = u; a[n - 1] = v
    x = link(rng, o, dep)
    x[:, 0::2, 0] = V - 1; x[:, 0::2, n - 1] = 0
    for g in range(1, 8, 2):
        m = (dep[:, g] == 0) & (rng.random((N, n)) < 0.5)
        x[:, g] = np.where(m, rng.integers(0, 2, (N, n)) * (V - 1), x[:, g])
    return pack(o, x, 255 * rng.integers(0, 2, (N, 8, n)))
def setup_inputs_spread(rng):
    z = np.maximum(Z >> rng.integers(0, 7, (N, 8)), 1); h = z + np.maximum((C - Z) >> rng.integers(0, 7, (N, 8)), W - 2)
    o = np.stack([np.stack([(rng.integers(0, V) + rng.permutation(n + n // 8)[:n]) % V for g in range(8)]) for r in range(N)]).astype(np.int64)
    o[:, 1::2] = np.sort(o[:, 1::2], axis=2)
    dep = depths(rng, counts(rng, h, z))
    return pack(o, link(rng, o, dep), 255 >> rng.integers(0, 9, (N, 8, n)))
def followers(o, x):
    to = np.zeros((N, 8, n), np.int64)
    for r in range(N):
        for g in range(8):
            where = np.full(V, -1, np.int64); where[o[(r + 1) % N, g]] = np.arange(n); to[r, g] = where[x[r, g]]
    return to
def step(p, v, t):
    return np.take_along_axis(np.roll(v, -t, axis=0), p, axis=2)
def chains(to, s):
    p = np.broadcast_to(np.arange(n), (N, 8, n)); tot = s.astype(np.int64)
    for t in range(1, W):
        p = np.where(p >= 0, step(np.maximum(p, 0), to, t - 1), -1)
        tot = tot + np.where(p >= 0, step(np.maximum(p, 0), s, t), 0)
    return p, tot
def check_inputs(d):
    try:
        o = np.stack([gentries(a) for a in d["own"]]).astype(np.int64); x = np.stack([gentries(a) for a in d["nxt"]]).astype(np.int64); s = np.asarray(d["pts"]).astype(np.int64)
        if o.shape != (N, 8, n) or x.shape != (N, 8, n) or s.shape != (N, 8, n): return ["shapes"]
        bad = []
        if s.min() < 0 or s.max() > 255: bad.append("points")
        if o.min() < 0 or o.max() >= V or x.min() < 0 or x.max() >= V: return bad + ["names in range"]
        if (np.diff(np.sort(o, axis=2), axis=2) == 0).any(): return bad + ["own names differ"]
        to = followers(o, x); p, tot = chains(to, s)
        if np.max(np.count_nonzero(to >= 0, axis=2)) > C: bad.append("followers")
        if np.max(np.count_nonzero(p >= 0, axis=2)) > Z: bad.append("kept")
        return bad
    except Exception:
        return ["shapes"]
def reference(own, nxt, pts):
    o = np.stack([gentries(a) for a in own]).astype(np.int64); x = np.stack([gentries(a) for a in nxt]).astype(np.int64)
    p, tot = chains(followers(o, x), pts)
    yk = np.full((N, 8, Z), -1, np.float32); ys = np.zeros((N, 8, Z), np.float32)
    for r in range(N):
        for g in range(8):
            i = np.flatnonzero(p[r, g] >= 0)
            yk[r, g, :len(i)] = o[r, g, i]; ys[r, g, :len(i)] = tot[r, g, i]
    return {"yk": yk, "ys": ys}

@@ -1,0 +1,456 @@
+from concourse.mybir import AluOpType as A, ActivationFunctionType as F
+
+BF, F32, F16, I32, U16 = "bfloat16", "float32", "float16", "int32", "uint16"
+SCRATCH = {
+    "own_i": ("sbuf", [128, 256], I32), "nxt_i": ("sbuf", [128, 256], I32), "pts_i": ("sbuf", [128, 256], I32),
+    "own_u": ("sbuf", [128, 256], U16), "nxt_u": ("sbuf", [128, 256], U16), "own_r": ("sbuf", [128, 256], U16),
+    "onh": ("sbuf", [128, 256], BF), "nmb": ("sbuf", [128, 512], BF),
+    "ptsb": ("sbuf", [128, 256], BF), "zb": ("sbuf", [128, 1028], BF),
+    "tab": ("sbuf", [128, 16384], BF), "dat": ("sbuf", [128, 4096], BF), "gat": ("sbuf", [128, 4096], BF),
+    "pidx": ("sbuf", [128, 1], I32), "par": ("sbuf", [128, 1], I32), "p16": ("sbuf", [128, 1], I32),
+    "colA": ("sbuf", [128, 1], F32), "colB": ("sbuf", [128, 1], F32), "colF": ("sbuf", [128, 1], F32),
+    "colU": ("sbuf", [128, 1], F32), "colN": ("sbuf", [128, 1], F32), "totm": ("sbuf", [128, 1], F32),
+    "lb0": ("sbuf", [128, 16], F32), "lb": ("sbuf", [128, 16], F32),
+    "bl": ("sbuf", [128, 256], BF), "bh": ("sbuf", [128, 256], BF), "bx": ("sbuf", [128, 256], BF),
+    "by": ("sbuf", [128, 256], BF), "bs": ("sbuf", [128, 256], BF),
+    "cz": ("sbuf", [128, 2176], BF),
+    "z1": ("sbuf", [128, 144], F16), "zx": ("sbuf", [128, 144], F16), "t32": ("sbuf", [1, 256], BF),
+    "c32": ("sbuf", [1, 256], BF),
+    "mrow": ("sbuf", [128, 1024], F32), "cio": ("sbuf", [128, 256], BF), "rw": ("sbuf", [128, 64], F32),
+    "sl": ("sbuf", [128, 64], F32), "tk": ("sbuf", [128, 64], F32), "thr": ("sbuf", [128, 64], F32),
+    "mk": ("sbuf", [128, 1280], BF), "pr8": ("sbuf", [8, 4096], BF), "pt": ("sbuf", [128, 256], BF),
+    "ng": ("sbuf", [128, 1024], BF), "hl": ("sbuf", [128, 512], BF),
+    "p5": ("sbuf", [128, 256], F32), "cd": ("sbuf", [128, 256], F32),
+    "fl": ("sbuf", [128, 264], BF),
+    "ax": ("sbuf", [128, 257], F32), "o16": ("sbuf", [128, 256], F16), "wq": ("sbuf", [128, 256], F32),
+    "ol": ("sbuf", [128, 16], U16), "cm": ("sbuf", [128, 1024], BF), "l1": ("sbuf", [128, 64], U16),
+    "sel": ("sbuf", [128, 1024], BF), "hls": ("sbuf", [128, 1024], F16),
+    "ll": ("sbuf", [128, 128], U16), "l3": ("sbuf", [128, 64], U16), "l4": ("sbuf", [128, 64], U16),
+    "l5": ("sbuf", [128, 64], U16),
+    "tb1": ("sbuf", [128, 4112], BF), "tb2": ("sbuf", [128, 4112], BF),
+    "r1": ("sbuf", [128, 1024], BF), "r2": ("sbuf", [128, 1024], BF), "r3": ("sbuf", [128, 1024], F32),
+    "fl4": ("sbuf", [128, 72], BF), "xn": ("sbuf", [128, 64], F32), "xx": ("sbuf", [128, 64], F32),
+    "a4": ("sbuf", [128, 64], F32), "o4": ("sbuf", [128, 64], F32),
+    "fd": ("sbuf", [128, 1024], F32), "win": ("sbuf", [128, 1408], F32),
+    "lpt1": ("dram", [128, 256], BF), "lpt2": ("dram", [128, 256], BF), "lpt3": ("dram", [128, 256], BF),
+    "lhl1": ("dram", [128, 512], BF), "lhl2": ("dram", [128, 512], BF),
+}
+for _b in range(8):
+    SCRATCH["ps%d" % _b] = ("psum", [128, 512], F32)
+NE = 138
+SEMAPHORES = ["own_r_s", "lpt1_s", "lpt2_s", "lpt3_s", "lhl1_s", "lhl2_s", "ls"] + ["e%d" % _i for _i in range(NE)]
+
+I1, I256 = 0, 2048
+ZW, ZN, EP, Z1, ZX, ZU = 144, 288, 432, 576, 720, 864
+FS, ON4, DG, FO, FT, FP, FN, FR = 1024, 1152, 1280, 1408, 1536, 1664, 1792, 1920
+TG0, TG, TD, TS = 384, 1408, 2048, 6656
+AE = 1536
+N0, N1, R1, R2 = 20, 36, 36, 36
+B0 = 192.0
+BW = 256.0 * B0
+
+
+def rank_program(g, core, T, topo):
+    r = T.rank_of(core)
+    if r is None:
+        return
+    n = len(T.cores)
+    d1, d2, d3 = (T.cores[(r - k) % n] for k in (1, 2, 3))
+    s1, s2, s3 = (T.cores[(r + k) % n] for k in (1, 2, 3))
+    V, S, P, Y = g.vector, g.scalar, g.tensor, g.sync
+    Q = {"g": g, "v": V, "s": S, "p": P, "y": Y}
+    ctr, seen, waited, made, ls = [0], {}, {}, [], [0]
+
+    def new():
+        t = ["e%d" % ctr[0], 0]
+        ctr[0] += 1
+        made.append(t)
+        return t
+
+    def sig(ins, t=None, by=1):
+        t = t or new()
+        ins.then_inc(T.sem[t[0]], by)
+        t[1] += by
+        return t
+
+    def dsig(ins, t=None):
+        return sig(ins, t, 16)
+
+    def w(q, *toks):
+        for t in toks:
+            if seen.get((q, t[0]), 0) < t[1]:
+                Q[q].wait_ge(T.sem[t[0]], t[1])
+                seen[(q, t[0])] = t[1]
+                waited[t[0]] = t[1]
+
+    def landed(q, nm, src):
+        Q[q].wait_ge(T.sem[nm], len(topo.engines(src, core)))
+
+    def send(dst, out, in_, sem):
+        rid, pid = topo.addr(dst)[:2]
+        eng = topo.engines(core, dst)
+        g.remote_dma(out_ap=out, in_ap=in_, remote_sem=T.sem[sem], local_sem=T.sem.ls, pid=pid, routing_id=rid,
+                     dma_engine_mask=sum(1 << e for e in eng))
+        ls[0] += len(eng)
+
+    def iota(out, pattern, base=0, cm=0):
+        return g.iota(out, pattern, base, cm, allow_small_or_imprecise_dtypes=True)
+
+    def cz(b, width=128, rows=128):
+        return T.cz[0:rows, b:b + width]
+
+    def mm(out, lhsT, rhs, first, last):
+        return P.matmul(out, lhsT, rhs, first, last)
+
+    ps = [T["ps%d" % b] for b in range(8)]
+
+    t_own = dsig(Y.dma_start(T.own_i[:, :], T.own[:, :]))
+    t_nxt = dsig(S.dma_start(T.nxt_i[:, :], T.nxt[:, :]))
+    t_pts = dsig(Y.dma_start(T.pts_i[:, :], T.pts[:, :]))
+
+    k0, k1, k5 = new(), new(), new()
+    f_tab, f_tabv, t_tab, t_cz = new(), new(), new(), new()
+    sig(g.iota(T.pidx[:, :], [[0, 1]], 0, 1), k0)
+    sig(iota(T.lb0[:, :], [[16, 16]]), k0)
+    sig(iota(T.bl[:, :], [[1, 16], [0, 16]]), k1)
+    sig(iota(T.bh[:, :], [[0, 16], [1, 16]]), k1)
+    sig(iota(T.tab[:, 0:TG0], [[0, TG0]]), f_tab)
+
+    z0 = sig(V.memset(T.zb[:, :], 0.0))
+    w("s", z0)
+    for a in range(TG + TD, TG + TD + TS, 1024):
+        b = min(a + 1024, TG + TD + TS)
+        sig(S.activation(T.tab[:, a:b], T.zb[:, 0:b - a], F.Copy), f_tab)
+    w("y", z0)
+    for a in range(TG, TG + TD, 1024):
+        dsig(Y.dma_start(T.tab[:, a:a + 1024], T.zb[:, 0:1024]), t_tab)
+    for a in (0, 1024):
+        dsig(Y.dma_start(T.cz[:, a:a + 1024], T.zb[:, 0:1024]), t_cz)
+    V0 = TG + TD + TS
+    VE = V0 + 2048
+    sig(V.memset(T.tab[:, V0:VE], 0.0), f_tabv)
+
+    w("v", k0)
+    c1, cc = new(), new()
+    sig(V.tensor_scalar(T.par[:, :], T.pidx[:, :], 1, None, A.bitwise_and), c1)
+    sig(V.tensor_scalar(T.p16[:, :], T.pidx[:, :], 15, None, A.bitwise_and), c1)
+    w("v", c1)
+    sig(V.tensor_copy(T.colB[:, :], T.par[:, :]), cc)
+    sig(V.tensor_scalar(T.colA[:, :], T.par[:, :], 0, None, A.is_equal), cc)
+    w("v", cc, k1)
+    b1 = new()
+    sig(V.tensor_scalar(T.lb[:, :], T.lb0[:, :], T.colB[:, :], None, A.mult), b1)
+    sig(V.tensor_scalar(T.bx[:, :], T.bl[:, :], T.colB[:, :], 1.0, A.mult, A.add), b1)
+    sig(V.tensor_scalar(T.by[:, :], T.bh[:, :], T.colA[:, :], None, A.mult), b1)
+    w("v", t_own)
+    c_own = sig(V.tensor_copy(T.own_u[:, :], T.own_i[:, :]))
+    w("v", b1)
+    b2 = sig(V.tensor_tensor(T.bs[:, :], T.bx[:, :], T.by[:, :], A.add))
+    w("v", b2)
+    da, db = new(), new()
+    for ch in range(AE // 256):
+        sig(V.tensor_scalar(T.dat[:, 256 * ch:256 * ch + 256], T.bs[:, :], T.lb[:, ch:ch + 1], None, A.add), da)
+    w("v", t_pts)
+    c_pts = sig(V.tensor_copy(T.ptsb[:, :], T.pts_i[:, :]))
+    w("v", t_nxt)
+    c_nxt = sig(V.tensor_copy(T.nxt_u[:, :], T.nxt_i[:, :]))
+    sig(V.memset(T.tab[:, VE:16384], 0.0), f_tabv)
+    w("s", b1, b2)
+    for ch in range(AE // 256, 16):
+        sig(S.activation(T.dat[:, 256 * ch:256 * ch + 256], T.bs[:, :], F.Identity, bias=T.lb[:, ch:ch + 1]), db)
+
+    w("g", c_own)
+    send(d1, T.own_r[:, :], T.own_u[:, :], "own_r_s")
+    sig(iota(T.tab[:, TG0:TG], [[0, TG - TG0]]), f_tab)
+    sig(iota(T.cio[:, :], [[1, 256]]), k5)
+    k6, km, ks, zz = new(), new(), new(), new()
+    sig(iota(T.mrow[:, 0:128], [[1, 128]], 2049), km)
+    sig(iota(T.rw[:, :], [[16, 64]], 264, 1), k6)
+
+    w("v", f_tab, f_tabv, t_tab, da)
+    landed("v", "own_r_s", s1)
+    t_s0 = sig(V.tensor_copy(T.tab[:, :].indirect(T.own_r[:, 0:AE // 16]), T.dat[:, 0:AE]))
+    w("v", db, t_s0)
+    t_sc = sig(V.tensor_copy(T.tab[:, :].indirect(T.own_r[:, AE // 16:256]), T.dat[:, AE:4096]))
+
+    w("y", c_pts)
+    t_pr8 = dsig(Y.dma_start(T.pr8[:, :], T.ptsb[:, :]))
+    t_tb = new()
+    for tb in (T.tb1, T.tb2):
+        for a in range(0, 4112, 1028):
+            dsig(Y.dma_start(tb[:, a:a + 1028], T.zb[:, :]), t_tb)
+
+    def view(b, start):
+        return T.cz[:, b + start:b + start + 113:16]
+
+    def put(x, part, wt):
+        return g.affine_select(x, x, [[-16, 8]], A.not_equal, wt, -part, 1)
+
+    def setw(x, pattern, wt, base, cm):
+        return g.affine_select(x, x, pattern, A.is_ge, wt, base, cm)
+    k2, k3, k4, kf, kz = new(), new(), new(), new(), new()
+    ep = T.cz[0:8, EP + 15:EP + 128:16]
+    grp = [[16, 8], [0, 16]]
+    vx = view(ZX, 15)
+    w("g", t_cz)
+    sig(g.affine_select(ep, ep, [[-1, 8]], A.not_equal, 1.0, 0, 1), k2)
+    sig(put(view(ZN, 15), 0, 1024.0), kz)
+    w("g", kz)
+    sig(put(view(ZN, 15), 1, 1.0), kz)
+    sig(setw(cz(FO), grp, 1.0, -1, -1), kf)
+    w("g", kf)
+    sig(setw(cz(FO), grp, 0.0, 15, -1), kf)
+    sig(put(view(Z1, 15), 0, 1.0), k3)
+    sig(setw(vx, [[16, 8]], 1.0, -1, -1), k3)
+    sig(put(view(ZW, 15), 0, 256.0), k3)
+    sig(put(view(FN, 8), 4, 128.0), k3)
+    w("g", kf)
+    sig(g.affine_select(cz(FT), cz(FO), [[1, 128]], A.is_ge, 0.0, 0, -1), k4)
+    sig(g.affine_select(cz(FS), cz(FO), [[-1, 128]], A.is_gt, 0.0, 0, 1), k4)
+    ki = sig(g.affine_select(cz(I1), cz(I1), [[-1, 128]], A.not_equal, 1.0, 0, 1))
+    sig(put(view(FP, 9), 2, 1.0), k4)
+    sig(put(view(FR, 9), 9, 1.0), k4)
+    sig(put(view(FN, 9), 6, 1.0), k4)
+    w("g", k3)
+    sig(setw(vx, [[16, 8]], 0.0, 15, -1), k4)
+    sig(put(view(ZW, 15), 1, 1.0), k4)
+    sig(put(view(FN, 8), 5, 1.0), k4)
+
+    kr = new()
+    sig(S.activation(T.t32[:, :], T.zb[0:1, 0:256], F.Identity, bias=32.0), kr)
+    sig(S.activation(T.fl[:, 0:8], T.zb[:, 0:8], F.Copy), zz)
+    sig(S.activation(T.fl4[:, 0:8], T.zb[:, 0:8], F.Copy), zz)
+    w("s", k5)
+    sig(S.activation(T.c32[:, :], T.cio[0:1, :], F.Copy, scale=1.0 / 32), kr)
+    for b in (128, 256, 512):
+        w("s", km)
+        sig(S.activation(T.mrow[:, b:2 * b], T.mrow[:, 0:b], F.Identity, bias=float(b)), km)
+    w("s", km)
+    sig(S.activation(T.sl[:, :], T.mrow[:, 0:1024:16], F.Identity, bias=-2049.0), ks)
+    w("p", t_pr8, k2)
+    for kk in range(16):
+        m = mm(ps[2][:, 0:256], cz(EP + 15 - kk, 128, 8), T.pr8[:, kk:4096:16], kk == 0, kk == 15)
+    m_pt = sig(m)
+    w("s", m_pt)
+    c_pt = sig(S.activation(T.pt[:, :], ps[2][:, 0:256], F.Copy))
+    w("s", kf)
+    sig(S.activation(cz(ON4), cz(FO), F.Copy, scale=-2048.0), kr)
+    w("s", ki)
+    sig(S.activation(cz(DG), cz(I1), F.Copy, scale=2048.0), kr)
+    sig(S.activation(cz(I256), cz(I1), F.Copy, scale=256.0), kr)
+    w("g", c_pt)
+    send(d1, T.lpt1[:, :], T.pt[:, :], "lpt1_s")
+    send(d2, T.lpt2[:, :], T.pt[:, :], "lpt2_s")
+    send(d3, T.lpt3[:, :], T.pt[:, :], "lpt3_s")
+    t_mk = sig(iota(T.mk[:, 0:1024], [[0, 1024]]))
+    tab0, tab1, tab2 = new(), new(), new()
+    w("y", c_pt, t_sc)
+    dsig(Y.dma_start(T.dat[6:128:16, :], T.pt[:, :]), tab0)
+    w("y", t_tb)
+    landed("y", "lpt1_s", s1)
+    dsig(Y.dma_start(T.tb1[2:128:16, 16:4112], T.lpt1[:, :]), tab1)
+    landed("y", "lpt2_s", s2)
+    dsig(Y.dma_start(T.tb2[9:128:16, 16:4112], T.lpt2[:, :]), tab2)
+    landed("y", "lpt3_s", s3)
+    dsig(Y.dma_start(T.tb1[9:128:16, 16:4112], T.lpt3[:, :]), tab1)
+
+    w("s", t_sc, c_nxt)
+    w("v", t_sc, c_nxt)
+    gt = []
+    for j in range(4):
+        t = new()
+        for hh in range(2):
+            a = 1024 * j + 512 * hh
+            o, src = T.gat[:, a:a + 512], T.tab[:, :].indirect(T.nxt_u[:, a // 16:a // 16 + 32])
+            sig(S.activation(o, src, F.Copy) if hh else V.tensor_copy(o, src), t)
+        gt.append(t)
+    m_cd = [new(), new()]
+    w("p", kr)
+    mm(ps[3][:, 0:256], T.t32[:, 0:128], T.t32[:, :], True, False)
+    mm(ps[3][:, 0:256], T.t32[:, 0:128], T.c32[:, :], False, False)
+    w("p", kz)
+    for j in range(4):
+        w("p", gt[j])
+        for kk in range(16):
+            m = mm(ps[6 + j // 2][:, 64 * (j % 2):64 * (j % 2) + 64], cz(ZN + 15 - kk),
+                   T.gat[:, 1024 * j + kk:1024 * j + 1024:16], kk == 0, kk == 15)
+        sig(m, m_cd[j // 2])
+
+    w("v", m_cd[0])
+    f_l, f_l0 = new(), new()
+    sig(V.tensor_scalar(T.fl[:, 8:136], ps[6][:, 0:128], 0.0, None, A.is_gt), f_l0)
+    hlc, x1, c_p5, nm1 = new(), new(), new(), new()
+    nm0 = sig(V.tensor_scalar(T.onh[:, :], T.own_i[:, :], 1.0 / 128, 128.0, A.mult, A.add))
+
+    def first(hh, fl_):
+        w("s", m_cd[hh], fl_)
+        x = sig(S.activation(T.hl[:, 128 * hh:128 * hh + 128], ps[6 + hh][:, 0:128], F.Identity, bias=B0, scale=1.0 / 1024), x1)
+        w("s", x)
+        sig(S.activation(T.p5[:, 128 * hh:128 * hh + 128], T.hl[:, 128 * hh:128 * hh + 128], F.Identity, bias=-1024.0 * B0,
+                         scale=1024.0), c_p5)
+
+    def second(hh):
+        w("v", c_p5)
+        sig(V.tensor_tensor(T.hl[:, 256 + 128 * hh:384 + 128 * hh], ps[6 + hh][:, 0:128], T.p5[:, 128 * hh:128 * hh + 128],
+                            A.subtract), hlc)
+    first(0, f_l0)
+    second(0)
+    w("s", nm0)
+    n128 = sig(S.activation(ps[1][:, 0:256], T.onh[:, :], F.Identity, bias=-16384.0, scale=128.0))
+    w("v", m_cd[1])
+    sig(V.tensor_scalar(T.fl[:, 136:264], ps[7][:, 0:128], 0.0, None, A.is_gt), f_l)
+    w("v", k3)
+    z1h = sig(V.tensor_copy(T.z1[:, :], cz(Z1, 144)))
+    first(1, f_l)
+    sig(S.activation(T.nmb[:, 0:256], T.onh[:, :], F.Identity, bias=-128.0), nm1)
+    w("p", f_l0, f_l, zz, c_pt, kf, k3, k4)
+    m_c = sig(mm(ps[2][:, 0:257], cz(FO), T.fl[:, 7:264], True, True))
+    m_x = sig(mm(ps[3][:, 0:256], cz(ON4), T.fl[:, 8:264], False, True))
+    w("v", m_c, z0)
+    ta = sig(V.tensor_tensor_scan(T.ax[:, :], ps[2][:, 0:257], T.zb[:, 0:257], 0.0, A.add, A.add))
+    w("v", ta, m_x)
+    to = sig(V.tensor_tensor(T.o16[:, :], T.ax[:, 0:256], ps[3][:, 0:256], A.max))
+    second(1)
+    w("p", z1h, to)
+    for k in range(16):
+        m = mm(ps[5][:, 0:16], T.z1[:, 15 - k:143 - k], T.o16[:, k:256:16], k == 0, k == 15)
+    m_o = sig(m)
+    mm(ps[4][:, 0:256], cz(FT), T.fl[:, 8:264], True, False)
+    m_p = sig(mm(ps[4][:, 0:256], cz(DG), T.fl[:, 8:264], False, True))
+    w("p", x1, hlc)
+    mm(ps[0][:, 0:256], cz(I256), T.hl[:, 0:256], True, False)
+    m_cp = sig(mm(ps[0][:, 0:256], cz(I1), T.hl[:, 256:512], False, True))
+    w("s", m_cp)
+    tcd = sig(S.activation(T.cd[:, :], ps[0][:, 0:256], F.Identity, bias=-2304.0 - BW))
+    w("g", x1, hlc)
+    send(d1, T.lhl1[:, :], T.hl[:, :], "lhl1_s")
+    send(d2, T.lhl2[:, :], T.hl[:, :], "lhl2_s")
+    cu = new()
+    sig(V.tensor_scalar(T.colU[:, :], T.p16[:, :], 256.0, None, A.mult), cu)
+    w("v", n128)
+    sig(V.tensor_tensor(T.nmb[:, 256:512], T.own_i[:, :], ps[1][:, 0:256], A.subtract), nm1)
+    w("s", nm1, t_sc)
+    dsig(S.dma_start(T.dat[4:128:16, :], T.nmb[:, 0:256]), tab0)
+    dsig(S.dma_start(T.dat[5:128:16, :], T.nmb[:, 256:512]), tab0)
+    w("v", m_o)
+    tol = sig(V.tensor_copy(T.ol[:, :], ps[5][:, 0:16]))
+    w("v", tol, t_mk, k5)
+    tmk = sig(V.tensor_copy(T.mk[:, :].indirect(T.ol[:, :]), T.cio[:, :]))
+    w("v", tmk)
+    tcm = sig(V.tensor_tensor_scan(T.cm[:, :], T.mk[:, 0:1024], T.zb[:, 0:1024], 0.0, A.max, A.max))
+    w("p", tcm)
+    for k in range(16):
+        m = mm(ps[5][:, 64:128], cz(Z1 + 15 - k), T.cm[:, k:1024:16], k == 0, k == 15)
+    m_l1 = sig(m)
+    for k in range(16):
+        mm(ps[2][:, 0:64], cz(Z1 + 15 - k), T.cm[:, k:1024:16], k == 0, False)
+    w("v", m_p)
+    twq = sig(V.tensor_tensor(T.wq[:, :], T.ax[:, 0:256], ps[4][:, 0:256], A.add))
+    w("v", k4)
+    zxh = sig(V.tensor_copy(T.zx[:, :], cz(ZX, 144)))
+    w("v", m_l1)
+    tl1 = sig(V.tensor_copy(T.l1[:, :], ps[5][:, 64:128]))
+    w("v", tl1, twq, km)
+    tse = sig(V.tensor_tensor(T.sel[:, :], T.wq[:, :].indirect(T.l1[:, :]), T.mrow[:, :], A.is_equal))
+    for tb, ld, sm, src, tok in ((T.tb1, T.lhl1, "lhl1_s", s1, tab1), (T.tb2, T.lhl2, "lhl2_s", s2, tab2)):
+        landed("y", sm, src)
+        for s_ in range(2):
+            dsig(Y.dma_start(tb[s_:128:16, 16:4112], ld[:, 256 * s_:256 * s_ + 256]), tok)
+
+    w("s", k4, cu)
+    ksc, fw, ttm, cv = new(), new(), new(), new()
+    sig(S.activation(view(ZU, 15), vx, F.Copy, scale=T.colU[:, :]), ksc)
+    w("p", tse, ksc)
+    for k in range(16):
+        m = mm(ps[2][:, 0:64], cz(ZU + 15 - k), T.sel[:, k:1024:16], False, k == 15)
+    m_lo = sig(m)
+    w("v", tse, tcd)
+    ths = sig(V.tensor_tensor(T.hls[:, :], T.cd[:, :].indirect(T.l1[:, :]), T.sel[:, :], A.mult))
+    w("p", ths, zxh)
+    for k in range(16):
+        m = mm(ps[5][:, 128:192], T.zx[:, 15 - k:143 - k], T.hls[:, k:1024:16], k == 0, k == 15)
+    m_l2 = sig(m)
+    tll0, tll = new(), new()
+    w("v", m_lo)
+    sig(V.tensor_copy(T.ll[:, 64:128], ps[2][:, 0:64]), tll0)
+    sig(V.tensor_scalar(T.colN[:, :], T.p16[:, :], -1.0, None, A.mult), cv)
+    sig(V.tensor_scalar(T.colF[:, :], T.p16[:, :], 8, -1.0, A.is_equal, A.mult), cv)
+
+    def pick(q, tb, lst, at, u, v, out, tok, *toks):
+        w(q, *toks)
+        src, o = tb[:, :].indirect(lst[:, at + u:at + v]), out[:, 16 * u:16 * v]
+        sig(V.tensor_copy(o, src) if q == "v" else S.activation(o, src, F.Copy), tok)
+    tng, tr1, tr2 = new(), new(), new()
+    pick("s", T.dat, T.ll, 64, 0, N0, T.ng, tng, tll0, tab0)
+    w("v", m_l2)
+    sig(V.tensor_scalar(T.ll[:, 0:64], ps[5][:, 128:192], 2063.0, None, A.add), tll)
+    pick("v", T.tb1, T.ll, 0, 0, R1, T.r1, tr1, tll, tab1)
+    pick("s", T.tb1, T.ll, 0, R1, 64, T.r1, tr1, tll, tab1)
+    pick("v", T.dat, T.ll, 64, N0, N1, T.ng, tng, tll0, tab0)
+    pick("s", T.dat, T.ll, 64, N1, 64, T.ng, tng, tll0, tab0)
+    w("p", tcd, nm1, tll, tr1)
+    for k in range(16):
+        m = mm(ps[1][:, 0:64], cz(ZW + 15 - k), T.r1[:, k:1024:16], k == 0, k == 15)
+    m_l3 = sig(m)
+    w("p", hlc, tng)
+    mm(ps[6][:, :], cz(FN), T.ng[:, 0:512], True, False)
+    m_ac = sig(mm(ps[6][:, :], cz(FP), T.r1[:, 0:512], False, True))
+    w("s", ta, cv)
+    sig(S.activation(T.totm[:, :], T.ax[:, 256:257], F.Identity, bias=T.colN[:, :]), ttm)
+    sig(S.activation(T.win[:, 0:264], T.zb[:, 0:264], F.Identity, bias=T.colF[:, :]), fw)
+    w("v", m_l3)
+    tl3 = sig(V.tensor_scalar(T.l3[:, :], ps[1][:, 0:64], -241.0 - BW, None, A.add))
+    pick("v", T.tb2, T.l3, 0, 0, R2, T.r2, tr2, tl3, tab2)
+    pick("s", T.tb2, T.l3, 0, R2, 64, T.r2, tr2, tl3, tab2)
+    w("v", ttm, ks)
+    ttk = sig(V.tensor_scalar(T.tk[:, :], T.sl[:, :], T.totm[:, :], None, A.is_ge))
+    w("s", ttk)
+    tth = sig(S.activation(T.thr[:, :], T.tk[:, :], F.Copy, bias=BW, scale=8192.0))
+    w("p", tr2)
+    for k in range(16):
+        m = mm(ps[0][:, 256:320], cz(ZW + 15 - k), T.r2[:, k:1024:16], k == 0, k == 15)
+    m_l4 = sig(m)
+    w("v", m_ac, tr2)
+    tfd = [sig(V.tensor_tensor(T.fd[:, 0:512], ps[6][:, :], T.r2[:, 0:512], A.add))]
+
+    w("v", m_l4)
+    tl5 = sig(V.tensor_scalar(T.l5[:, :], ps[0][:, 256:320], -241.0 - BW, None, A.add))
+    w("v", tth)
+    f4 = sig(V.tensor_tensor(T.fl4[:, 8:72], ps[0][:, 256:320], T.thr[:, :], A.is_gt))
+    x2 = sig(V.tensor_tensor(T.xn[:, :], ps[0][:, 256:320], T.thr[:, :], A.is_le))
+    w("s", tl5)
+    tr3 = [sig(S.activation(T.r3[:, 512 * hh:512 * hh + 512], T.tb1[:, :].indirect(T.l5[:, 32 * hh:32 * hh + 32]), F.Copy))
+           for hh in range(2)]
+    mm(ps[7][:, :], cz(FN), T.ng[:, 512:1024], True, False)
+    w("p", f4, zz)
+    mm(ps[2][:, 0:64], cz(FS), T.fl4[:, 7:71], True, False)
+    m_a = sig(mm(ps[2][:, 0:64], cz(FT), T.fl4[:, 8:72], False, True))
+    mm(ps[7][:, :], cz(FP), T.r1[:, 512:1024], False, False)
+    m_ad = sig(mm(ps[7][:, :], cz(FR), T.r2[:, 512:1024], False, True))
+    w("s", m_ad)
+    tfd.append(sig(S.activation(T.fd[:, 512:1024], ps[7][:, :], F.Copy)))
+    w("v", x2, k6)
+    x3 = sig(V.tensor_tensor(T.xx[:, :], T.xn[:, :], T.rw[:, :], A.mult))
+    w("v", m_a)
+    q1 = sig(V.tensor_tensor_scan(T.a4[:, :], ps[2][:, 0:64], T.zb[:, 0:64], 0.0, A.add, A.add))
+    w("v", q1, x3)
+    q3 = sig(V.tensor_tensor(T.o4[:, :], T.a4[:, :], T.xx[:, :], A.max))
+    w("v", q3)
+    q5 = sig(V.tensor_copy(T.l4[:, :], T.o4[:, :]))
+    w("v", q5, fw)
+    tw = None
+    for hh in range(2):
+        w("v", tfd[hh], tr3[hh])
+        if tw:
+            w("v", tw)
+        tw = sig(V.tensor_tensor(T.win[:, :].indirect(T.l4[:, 32 * hh:32 * hh + 32]), T.fd[:, 512 * hh:512 * hh + 512],
+                                 T.r3[:, 512 * hh:512 * hh + 512], A.add))
+    w("y", tw)
+    t_y = new()
+    w("s", tw)
+    dsig(Y.dma_start(T.yk[:, :], T.win[8:128:16, 1:257]), t_y)
+    dsig(S.dma_start(T.ys[:, :], T.win[9:128:16, 1:257]), t_y)
+    for t in made:
+        if waited.get(t[0], 0) < t[1]:
+            w("y", t)
+    g.wait_ge(T.sem.ls, ls[0])

@@ -1,53 +1,52 @@
 from concourse.mybir import AluOpType as A, ActivationFunctionType as F
 
 BF, F32, F16, I32, U16 = "bfloat16", "float32", "float16", "int32", "uint16"
+TW = 4160
 SCRATCH = {
     "own_i": ("sbuf", [128, 256], I32), "nxt_i": ("sbuf", [128, 256], I32), "pts_i": ("sbuf", [128, 256], I32),
     "own_u": ("sbuf", [128, 256], U16), "nxt_u": ("sbuf", [128, 256], U16), "own_r": ("sbuf", [128, 256], U16),
-    "onh": ("sbuf", [128, 256], BF), "nmb": ("sbuf", [128, 512], BF),
-    "ptsb": ("sbuf", [128, 256], BF), "zb": ("sbuf", [128, 1028], BF),
-    "tab": ("sbuf", [128, 16384], BF), "dat": ("sbuf", [128, 4096], BF), "gat": ("sbuf", [128, 4096], BF),
-    "pidx": ("sbuf", [128, 1], I32), "par": ("sbuf", [128, 1], I32), "p16": ("sbuf", [128, 1], I32),
-    "colA": ("sbuf", [128, 1], F32), "colB": ("sbuf", [128, 1], F32), "colF": ("sbuf", [128, 1], F32),
-    "colU": ("sbuf", [128, 1], F32), "colN": ("sbuf", [128, 1], F32), "totm": ("sbuf", [128, 1], F32),
-    "lb0": ("sbuf", [128, 16], F32), "lb": ("sbuf", [128, 16], F32),
-    "bl": ("sbuf", [128, 256], BF), "bh": ("sbuf", [128, 256], BF), "bx": ("sbuf", [128, 256], BF),
-    "by": ("sbuf", [128, 256], BF), "bs": ("sbuf", [128, 256], BF),
-    "cz": ("sbuf", [128, 2176], BF),
-    "z1": ("sbuf", [128, 144], F16), "zx": ("sbuf", [128, 144], F16), "t32": ("sbuf", [1, 256], BF),
-    "c32": ("sbuf", [1, 256], BF),
-    "mrow": ("sbuf", [128, 1024], F32), "cio": ("sbuf", [128, 256], BF), "rw": ("sbuf", [128, 64], F32),
+    "nf": ("sbuf", [128, 256], F32), "onh": ("sbuf", [128, 256], BF), "nmb": ("sbuf", [128, 512], BF),
+    "ptsb": ("sbuf", [128, 256], BF), "zb": ("sbuf", [128, 1040], BF),
+    "tab": ("sbuf", [128, 16384], BF), "dat": ("sbuf", [128, TW], BF), "gat": ("sbuf", [128, TW], BF),
+    "pidx": ("sbuf", [128, 1], I32), "p16": ("sbuf", [128, 1], I32),
+    "colA": ("sbuf", [128, 1], F32), "colB": ("sbuf", [128, 1], F32), "colC": ("sbuf", [128, 1], F32),
+    "colF": ("sbuf", [128, 1], F32), "colN": ("sbuf", [128, 1], F32), "totm": ("sbuf", [128, 1], F32),
+    "io64": ("sbuf", [128, 64], BF), "lb": ("sbuf", [128, 64], F32),
+    "cz": ("sbuf", [128, 816], BF), "cy": ("sbuf", [128, 1536], BF), "i32": ("sbuf", [128, 128], F32),
+    "zm": ("sbuf", [128, 2048], BF), "ep": ("sbuf", [8, 144], BF), "zx": ("sbuf", [128, 288], F16),
+    "er": ("sbuf", [16, 272], BF), "ec": ("sbuf", [16, 256], BF), "el": ("sbuf", [16, 384], BF),
+    "d0": ("sbuf", [128, 256], BF), "c32": ("sbuf", [128, 1024], BF),
+    "cio": ("sbuf", [16, 256], BF), "cf": ("sbuf", [128, 256], F32), "rw": ("sbuf", [128, 64], F32),
     "sl": ("sbuf", [128, 64], F32), "tk": ("sbuf", [128, 64], F32), "thr": ("sbuf", [128, 64], F32),
-    "mk": ("sbuf", [128, 1280], BF), "pr8": ("sbuf", [8, 4096], BF), "pt": ("sbuf", [128, 256], BF),
-    "ng": ("sbuf", [128, 1024], BF), "hl": ("sbuf", [128, 512], BF),
-    "p5": ("sbuf", [128, 256], F32), "cd": ("sbuf", [128, 256], F32),
-    "fl": ("sbuf", [128, 264], BF),
-    "ax": ("sbuf", [128, 257], F32), "o16": ("sbuf", [128, 256], F16), "wq": ("sbuf", [128, 256], F32),
-    "ol": ("sbuf", [128, 16], U16), "cm": ("sbuf", [128, 1024], BF), "l1": ("sbuf", [128, 64], U16),
-    "sel": ("sbuf", [128, 1024], BF), "hls": ("sbuf", [128, 1024], F16),
+    "mk": ("sbuf", [128, 1280], F32), "wn": ("sbuf", [128, 1280], F32),
+    "pr8": ("sbuf", [8, 4096], BF), "pt": ("sbuf", [128, 256], BF),
+    "ng": ("sbuf", [128, 1024], BF), "nb": ("sbuf", [128, 272], BF),
+    "ax": ("sbuf", [128, 257], F32), "oy": ("sbuf", [128, 256], F16), "oh": ("sbuf", [128, 256], F16),
+    "wq": ("sbuf", [128, 256], F32), "ol": ("sbuf", [128, 16], U16), "cm": ("sbuf", [128, 1024], F16),
+    "dd": ("sbuf", [128, 1024], F16), "dc": ("sbuf", [128, 1024], F16),
+    "xi": ("sbuf", [128, 64], I32), "xp": ("sbuf", [128, 64], I32), "pb": ("sbuf", [128, 64], BF),
     "ll": ("sbuf", [128, 128], U16), "l3": ("sbuf", [128, 64], U16), "l4": ("sbuf", [128, 64], U16),
     "l5": ("sbuf", [128, 64], U16),
-    "tb1": ("sbuf", [128, 4112], BF), "tb2": ("sbuf", [128, 4112], BF),
     "r1": ("sbuf", [128, 1024], BF), "r2": ("sbuf", [128, 1024], BF), "r3": ("sbuf", [128, 1024], F32),
     "fl4": ("sbuf", [128, 72], BF), "xn": ("sbuf", [128, 64], F32), "xx": ("sbuf", [128, 64], F32),
     "a4": ("sbuf", [128, 64], F32), "o4": ("sbuf", [128, 64], F32),
     "fd": ("sbuf", [128, 1024], F32), "win": ("sbuf", [128, 1408], F32),
     "lpt1": ("dram", [128, 256], BF), "lpt2": ("dram", [128, 256], BF), "lpt3": ("dram", [128, 256], BF),
-    "lhl1": ("dram", [128, 512], BF), "lhl2": ("dram", [128, 512], BF),
+    "pst": ("dram", [128, 256], BF), "ost": ("dram", [3, 128, 256], BF), "st": ("dram", [2, 128, 256], BF), "la1": ("dram", [2, 128, 256], BF), "la2": ("dram", [2, 128, 256], BF),
 }
 for _b in range(8):
     SCRATCH["ps%d" % _b] = ("psum", [128, 512], F32)
 NE = 138
-SEMAPHORES = ["own_r_s", "lpt1_s", "lpt2_s", "lpt3_s", "lhl1_s", "lhl2_s", "ls"] + ["e%d" % _i for _i in range(NE)]
+SEMAPHORES = ["own_r_s", "lpt1_s", "lpt2_s", "lpt3_s", "la10", "la11", "la20", "la21", "ls"] + ["e%d" % _i for _i in range(NE)]
 
-I1, I256 = 0, 2048
-ZW, ZN, EP, Z1, ZX, ZU = 144, 288, 432, 576, 720, 864
-FS, ON4, DG, FO, FT, FP, FN, FR = 1024, 1152, 1280, 1408, 1536, 1664, 1792, 1920
-TG0, TG, TD, TS = 384, 1408, 2048, 6656
+ZN, ZX, Z1, FN, FP, FR = 0, 144, 288, 432, 560, 688
+CB = 32.0
+I4, IL, FO, WT, SO, WL, FT, FS, SL, ON4, IB, IC = (128 * _k for _k in range(12))
+TG0, TG, TD, TS = 640, 1792, 3072, 5632
+VA = (768, 768, 512)
 AE = 1536
-N0, N1, R1, R2 = 20, 36, 36, 36
-B0 = 192.0
-BW = 256.0 * B0
+N1, R1, R2 = 24, 36, 36
+RN, RS, RF = 10, 9, 12
 
 
 def rank_program(g, core, T, topo):
@@ -96,89 +95,113 @@ def rank_program(g, core, T, topo):
     def iota(out, pattern, base=0, cm=0):
         return g.iota(out, pattern, base, cm, allow_small_or_imprecise_dtypes=True)
 
-    def cz(b, width=128, rows=128):
-        return T.cz[0:rows, b:b + width]
+    def cz(b, width=128):
+        return T.cz[:, b:b + width]
+
+    def cy(b):
+        return T.cy[:, b:b + 128]
 
     def mm(out, lhsT, rhs, first, last):
         return P.matmul(out, lhsT, rhs, first, last)
 
+    def fold(out, mat, at_, rows_, last=True):
+        for k in range(16):
+            m = mm(out, mat[:, at_ + 15 - k:at_ + 143 - k], rows_[:, k:1024:16], k == 0, last and k == 15)
+        return sig(m) if last else None
+
     ps = [T["ps%d" % b] for b in range(8)]
 
     t_own = dsig(Y.dma_start(T.own_i[:, :], T.own[:, :]))
-    t_nxt = dsig(S.dma_start(T.nxt_i[:, :], T.nxt[:, :]))
     t_pts = dsig(Y.dma_start(T.pts_i[:, :], T.pts[:, :]))
+    t_nxt = dsig(Y.dma_start(T.nxt_i[:, :], T.nxt[:, :]))
 
-    k0, k1, k5 = new(), new(), new()
-    f_tab, f_tabv, t_tab, t_cz = new(), new(), new(), new()
+    k0, f_tab, f_tabv, t_tab = new(), new(), new(), new()
     sig(g.iota(T.pidx[:, :], [[0, 1]], 0, 1), k0)
-    sig(iota(T.lb0[:, :], [[16, 16]]), k0)
-    sig(iota(T.bl[:, :], [[1, 16], [0, 16]]), k1)
-    sig(iota(T.bh[:, :], [[0, 16], [1, 16]]), k1)
+    sig(iota(T.io64[:, :], [[1, 64]]), k0)
     sig(iota(T.tab[:, 0:TG0], [[0, TG0]]), f_tab)
 
-    z0 = sig(V.memset(T.zb[:, :], 0.0))
+    z00 = sig(V.memset(T.zb[:, 0:256], 0.0))
+    z0 = sig(V.memset(T.zb[:, 256:1040], 0.0))
+    w("s", z00)
+    a = TG + TD
+    for _ in range(2):
+        sig(S.activation(T.tab[:, a:a + 256], T.zb[:, 0:256], F.Copy), f_tab)
+        a += 256
     w("s", z0)
-    for a in range(TG + TD, TG + TD + TS, 1024):
+    for a in range(a, TG + TD + TS, 1024):
         b = min(a + 1024, TG + TD + TS)
         sig(S.activation(T.tab[:, a:b], T.zb[:, 0:b - a], F.Copy), f_tab)
-    w("y", z0)
+    w("y", z00, z0)
     for a in range(TG, TG + TD, 1024):
-        dsig(Y.dma_start(T.tab[:, a:a + 1024], T.zb[:, 0:1024]), t_tab)
-    for a in (0, 1024):
-        dsig(Y.dma_start(T.cz[:, a:a + 1024], T.zb[:, 0:1024]), t_cz)
-    V0 = TG + TD + TS
-    VE = V0 + 2048
-    sig(V.memset(T.tab[:, V0:VE], 0.0), f_tabv)
+        b = min(a + 1024, TG + TD)
+        dsig(Y.dma_start(T.tab[:, a:b], T.zb[:, 0:b - a]), t_tab)
+    at = [TG + TD + TS]
+
+    def zeros(width):
+        sig(V.memset(T.tab[:, at[0]:at[0] + width], 0.0), f_tabv)
+        at[0] += width
 
     w("v", k0)
-    c1, cc = new(), new()
-    sig(V.tensor_scalar(T.par[:, :], T.pidx[:, :], 1, None, A.bitwise_and), c1)
-    sig(V.tensor_scalar(T.p16[:, :], T.pidx[:, :], 15, None, A.bitwise_and), c1)
+    c1 = sig(V.tensor_scalar(T.p16[:, :], T.pidx[:, :], 15, None, A.bitwise_and))
+    zeros(VA[0])
     w("v", c1)
-    sig(V.tensor_copy(T.colB[:, :], T.par[:, :]), cc)
-    sig(V.tensor_scalar(T.colA[:, :], T.par[:, :], 0, None, A.is_equal), cc)
-    w("v", cc, k1)
-    b1 = new()
-    sig(V.tensor_scalar(T.lb[:, :], T.lb0[:, :], T.colB[:, :], None, A.mult), b1)
-    sig(V.tensor_scalar(T.bx[:, :], T.bl[:, :], T.colB[:, :], 1.0, A.mult, A.add), b1)
-    sig(V.tensor_scalar(T.by[:, :], T.bh[:, :], T.colA[:, :], None, A.mult), b1)
+    cc = new()
+    sig(V.tensor_scalar(T.colB[:, :], T.p16[:, :], 8, None, A.is_equal), cc)
+    sig(V.tensor_scalar(T.colA[:, :], T.p16[:, :], 0, None, A.is_equal), cc)
+    zeros(VA[1])
+    w("v", cc)
+    c2 = sig(V.tensor_scalar(T.colC[:, :], T.p16[:, :], RF, T.colA[:, :], A.is_equal, A.add))
     w("v", t_own)
     c_own = sig(V.tensor_copy(T.own_u[:, :], T.own_i[:, :]))
+    w("v", c2)
+    b1 = sig(V.tensor_scalar(T.lb[:, :], T.io64[:, :], T.colA[:, :], None, A.mult))
+    da = sig(V.tensor_scalar(T.dat[:, 64:128], T.io64[:, :], T.colB[:, :], T.colC[:, :], A.mult, A.add))
+    c_nf = sig(V.tensor_copy(T.nf[:, :], T.own_i[:, :]))
     w("v", b1)
-    b2 = sig(V.tensor_tensor(T.bs[:, :], T.bx[:, :], T.by[:, :], A.add))
-    w("v", b2)
-    da, db = new(), new()
-    for ch in range(AE // 256):
-        sig(V.tensor_scalar(T.dat[:, 256 * ch:256 * ch + 256], T.bs[:, :], T.lb[:, ch:ch + 1], None, A.add), da)
+
+    def double(to, frm, width):
+        w("v", da)
+        k = (to - frm) // 64
+        sig(V.tensor_scalar(T.dat[:, 64 + to:64 + to + width], T.dat[:, 64 + frm:64 + frm + width], T.lb[:, k:k + 1], None,
+                            A.add), da)
+    double(64, 0, 64)
+    zeros(VA[2])
+    double(128, 0, 128)
     w("v", t_pts)
     c_pts = sig(V.tensor_copy(T.ptsb[:, :], T.pts_i[:, :]))
+    double(256, 0, 256)
     w("v", t_nxt)
     c_nxt = sig(V.tensor_copy(T.nxt_u[:, :], T.nxt_i[:, :]))
-    sig(V.memset(T.tab[:, VE:16384], 0.0), f_tabv)
-    w("s", b1, b2)
-    for ch in range(AE // 256, 16):
-        sig(S.activation(T.dat[:, 256 * ch:256 * ch + 256], T.bs[:, :], F.Identity, bias=T.lb[:, ch:ch + 1]), db)
+    double(512, 0, 512)
+    zeros(512)
+    double(1024, 0, AE - 1024)
+    zeros(16384 - at[0])
+    db = new()
+    w("s", b1, da)
+    for to, frm, width in ((AE, AE - 1024, 2048 - AE), (2048, 0, 1024), (3072, 0, 1024)):
+        k = (to - frm) // 64
+        sig(S.activation(T.dat[:, 64 + to:64 + to + width], T.dat[:, 64 + frm:64 + frm + width], F.Identity,
+                         bias=T.lb[:, k:k + 1]), db)
 
     w("g", c_own)
     send(d1, T.own_r[:, :], T.own_u[:, :], "own_r_s")
     sig(iota(T.tab[:, TG0:TG], [[0, TG - TG0]]), f_tab)
-    sig(iota(T.cio[:, :], [[1, 256]]), k5)
-    k6, km, ks, zz = new(), new(), new(), new()
-    sig(iota(T.mrow[:, 0:128], [[1, 128]], 2049), km)
-    sig(iota(T.rw[:, :], [[16, 64]], 264, 1), k6)
 
     w("v", f_tab, f_tabv, t_tab, da)
     landed("v", "own_r_s", s1)
-    t_s0 = sig(V.tensor_copy(T.tab[:, :].indirect(T.own_r[:, 0:AE // 16]), T.dat[:, 0:AE]))
+    t_s0 = sig(V.tensor_copy(T.tab[:, :].indirect(T.own_r[:, 0:AE // 16]), T.dat[:, 64:64 + AE]))
     w("v", db, t_s0)
-    t_sc = sig(V.tensor_copy(T.tab[:, :].indirect(T.own_r[:, AE // 16:256]), T.dat[:, AE:4096]))
+    t_sc = sig(V.tensor_copy(T.tab[:, :].indirect(T.own_r[:, AE // 16:256]), T.dat[:, 64 + AE:TW]))
 
     w("y", c_pts)
-    t_pr8 = dsig(Y.dma_start(T.pr8[:, :], T.ptsb[:, :]))
-    t_tb = new()
-    for tb in (T.tb1, T.tb2):
-        for a in range(0, 4112, 1028):
-            dsig(Y.dma_start(tb[:, a:a + 1028], T.zb[:, :]), t_tb)
+    t_pst = dsig(Y.dma_start(T.pst[:, :], T.ptsb[:, :]))
+    w("y", t_pst)
+    t_pr8 = dsig(Y.dma_start(T.pr8[:, :], T.pst[:, :]))
+    landed("y", "own_r_s", s1)
+    t_zm = new()
+    for a in (0, 1024):
+        dsig(Y.dma_start(T.zm[:, a:a + 1024], T.zb[:, 0:1024]), t_zm)
+    t_cz = dsig(Y.dma_start(T.cz[:, :], T.zb[:, 0:816]))
 
     def view(b, start):
         return T.cz[:, b + start:b + start + 113:16]
@@ -186,73 +209,92 @@ def rank_program(g, core, T, topo):
     def put(x, part, wt):
         return g.affine_select(x, x, [[-16, 8]], A.not_equal, wt, -part, 1)
 
-    def setw(x, pattern, wt, base, cm):
-        return g.affine_select(x, x, pattern, A.is_ge, wt, base, cm)
-    k2, k3, k4, kf, kz = new(), new(), new(), new(), new()
-    ep = T.cz[0:8, EP + 15:EP + 128:16]
+    def setw(x, x0, pattern, wt, base, cm):
+        return g.affine_select(x, x0, pattern, A.is_ge, wt, base, cm)
     grp = [[16, 8], [0, 16]]
     vx = view(ZX, 15)
+    z128 = T.zb[:, 0:128]
+    kz, kf, k3, k4, k6, ki = new(), new(), new(), new(), new(), new()
+    w("g", z00, z0)
+    sig(setw(cy(FO), z128, grp, -32.0, -1, -1), kf)
+    sig(g.affine_select(cy(I4), z128, [[-1, 128]], A.not_equal, 0.25, 0, 1), ki)
+    w("g", kf)
+    sig(setw(cy(FO), cy(FO), grp, 0.0, 15, -1), kf)
+    sig(g.affine_select(cy(IL), z128, [[-1, 128]], A.not_equal, 1.0 / 256, 0, 1), ki)
+    w("g", kf)
+    kt = sig(g.affine_select(cy(WT), cy(FO), [[1, 128]], A.is_ge, 0.0, 0, -1))
+    k2 = sig(g.affine_select(T.ep[:, :], T.zb[0:8, 0:144], [[1, 144]], A.not_equal, 1.0, -15, -16))
+    w("g", t_pst)
+    send(d1, T.lpt1[:, :], T.pst[:, :], "lpt1_s")
+    send(d2, T.lpt2[:, :], T.pst[:, :], "lpt2_s")
+    send(d3, T.lpt3[:, :], T.pst[:, :], "lpt3_s")
+    kl = sig(g.affine_select(cy(WL), cy(FO), grp, A.is_equal, 0.0, 15, -1))
+    k5 = sig(iota(T.cio[:, :], [[1, 256]]))
+    ke = sig(g.affine_select(T.er[:, :], T.zb[0:16, 0:272], [[0, 17], [1, 16]], A.not_equal, 1.0, 0, -1))
+    w("g", k5)
+    kc = sig(g.affine_select(T.ec[:, :], T.cio[:, :], [[0, 16], [1, 16]], A.is_equal, 0.0, 0, -1))
     w("g", t_cz)
-    sig(g.affine_select(ep, ep, [[-1, 8]], A.not_equal, 1.0, 0, 1), k2)
-    sig(put(view(ZN, 15), 0, 1024.0), kz)
-    w("g", kz)
-    sig(put(view(ZN, 15), 1, 1.0), kz)
-    sig(setw(cz(FO), grp, 1.0, -1, -1), kf)
-    w("g", kf)
-    sig(setw(cz(FO), grp, 0.0, 15, -1), kf)
-    sig(put(view(Z1, 15), 0, 1.0), k3)
-    sig(setw(vx, [[16, 8]], 1.0, -1, -1), k3)
-    sig(put(view(ZW, 15), 0, 256.0), k3)
-    sig(put(view(FN, 8), 4, 128.0), k3)
-    w("g", kf)
-    sig(g.affine_select(cz(FT), cz(FO), [[1, 128]], A.is_ge, 0.0, 0, -1), k4)
-    sig(g.affine_select(cz(FS), cz(FO), [[-1, 128]], A.is_gt, 0.0, 0, 1), k4)
-    ki = sig(g.affine_select(cz(I1), cz(I1), [[-1, 128]], A.not_equal, 1.0, 0, 1))
-    sig(put(view(FP, 9), 2, 1.0), k4)
-    sig(put(view(FR, 9), 9, 1.0), k4)
-    sig(put(view(FN, 9), 6, 1.0), k4)
+    sig(setw(vx, vx, [[16, 8]], 256.0, -1, -1), k3)
+    sig(put(view(ZN, 15), 0, 0.25), k3)
+    sig(put(view(FN, RN), 4, 128.0), k3)
+    kx = sig(put(view(Z1, 15), 0, 1.0))
     w("g", k3)
-    sig(setw(vx, [[16, 8]], 0.0, 15, -1), k4)
-    sig(put(view(ZW, 15), 1, 1.0), k4)
-    sig(put(view(FN, 8), 5, 1.0), k4)
+    sig(setw(vx, vx, [[16, 8]], 0.0, 15, -1), kx)
+    kcf = sig(iota(T.cf[:, :], [[1, 256]], int(CB)))
+    kc32 = sig(iota(T.c32[:, :], [[0, 1024]], 32))
+    w("y", t_zm, ki, kt)
+    for part, b in ((0, I4), (8, IL), (RF, WT)):
+        dsig(Y.dma_start(T.zm[part:128:16, :], cy(b)), kz)
 
-    kr = new()
-    sig(S.activation(T.t32[:, :], T.zb[0:1, 0:256], F.Identity, bias=32.0), kr)
-    sig(S.activation(T.fl[:, 0:8], T.zb[:, 0:8], F.Copy), zz)
-    sig(S.activation(T.fl4[:, 0:8], T.zb[:, 0:8], F.Copy), zz)
-    w("s", k5)
-    sig(S.activation(T.c32[:, :], T.cio[0:1, :], F.Copy, scale=1.0 / 32), kr)
-    for b in (128, 256, 512):
-        w("s", km)
-        sig(S.activation(T.mrow[:, b:2 * b], T.mrow[:, 0:b], F.Identity, bias=float(b)), km)
-    w("s", km)
-    sig(S.activation(T.sl[:, :], T.mrow[:, 0:1024:16], F.Identity, bias=-2049.0), ks)
+    zz, nm1, kr = new(), new(), new()
     w("p", t_pr8, k2)
     for kk in range(16):
-        m = mm(ps[2][:, 0:256], cz(EP + 15 - kk, 128, 8), T.pr8[:, kk:4096:16], kk == 0, kk == 15)
+        m = mm(ps[4][:, 0:256], T.ep[:, 15 - kk:143 - kk], T.pr8[:, kk:4096:16], kk == 0, kk == 15)
     m_pt = sig(m)
-    w("s", m_pt)
-    c_pt = sig(S.activation(T.pt[:, :], ps[2][:, 0:256], F.Copy))
-    w("s", kf)
-    sig(S.activation(cz(ON4), cz(FO), F.Copy, scale=-2048.0), kr)
+    w("s", c_nf)
+    nm0 = sig(S.activation(T.onh[:, :], T.nf[:, :], F.Identity, bias=128.0, scale=1.0 / 128))
     w("s", ki)
-    sig(S.activation(cz(DG), cz(I1), F.Copy, scale=2048.0), kr)
-    sig(S.activation(cz(I256), cz(I1), F.Copy, scale=256.0), kr)
-    w("g", c_pt)
-    send(d1, T.lpt1[:, :], T.pt[:, :], "lpt1_s")
-    send(d2, T.lpt2[:, :], T.pt[:, :], "lpt2_s")
-    send(d3, T.lpt3[:, :], T.pt[:, :], "lpt3_s")
-    t_mk = sig(iota(T.mk[:, 0:1024], [[0, 1024]]))
-    tab0, tab1, tab2 = new(), new(), new()
-    w("y", c_pt, t_sc)
-    dsig(Y.dma_start(T.dat[6:128:16, :], T.pt[:, :]), tab0)
-    w("y", t_tb)
-    landed("y", "lpt1_s", s1)
-    dsig(Y.dma_start(T.tb1[2:128:16, 16:4112], T.lpt1[:, :]), tab1)
-    landed("y", "lpt2_s", s2)
-    dsig(Y.dma_start(T.tb2[9:128:16, 16:4112], T.lpt2[:, :]), tab2)
-    landed("y", "lpt3_s", s3)
-    dsig(Y.dma_start(T.tb1[9:128:16, 16:4112], T.lpt3[:, :]), tab1)
+    kb = new()
+    sig(S.activation(T.i32[:, :], cy(I4), F.Copy, scale=-128.0), kb)
+    sig(S.activation(cy(IB), cy(I4), F.Copy, scale=16384.0), kb)
+    sig(S.activation(T.nb[:, 0:8], T.zb[:, 0:8], F.Identity, bias=128.0), zz)
+    sig(S.activation(T.fl4[:, 0:8], T.zb[:, 0:8], F.Copy), zz)
+    sig(S.activation(T.dat[:, 0:64], T.zb[:, 0:64], F.Copy), zz)
+    sig(S.activation(T.gat[:, 0:64], T.zb[:, 0:64], F.Copy), zz)
+    w("s", nm0)
+    sig(S.activation(T.nmb[:, 0:256], T.onh[:, :], F.Identity, bias=-128.0), nm1)
+    sig(S.activation(T.el[:, 128:256], T.zb[0:16, 0:128], F.Identity, bias=262144.0), kr)
+    sig(S.activation(T.el[:, 256:384], T.zb[0:16, 0:128], F.Identity, bias=-128.0), kr)
+    w("s", m_pt)
+    c_pt = sig(S.activation(T.pt[:, :], ps[4][:, 0:256], F.Copy))
+    w("p", kb, nm0, c_nf)
+    mm(ps[5][:, 0:256], T.i32[:, :], T.nf[:, :], True, False)
+    m_nl = sig(mm(ps[5][:, 0:256], cy(IB), T.onh[:, :], False, True))
+    w("s", kl)
+    sig(S.activation(cy(ON4), cy(WL), F.Copy, scale=64.0), kr)
+    sig(S.activation(cy(SL), cy(WL), F.Copy, scale=-1.0 / 32), kr)
+    w("s", m_nl)
+    sig(S.activation(T.nmb[:, 256:512], ps[5][:, 0:256], F.Identity, bias=16384.0, scale=-1.0 / 32), nm1)
+    w("s", ke)
+    sig(S.activation(T.el[:, 0:128], T.er[:, 0:128], F.Identity, bias=41984.0, scale=-40960.0), kr)
+    w("p", c_pt, ke)
+    m_d0 = sig(mm(ps[4][:, 0:256], T.er[:, 0:128], T.er[:, 0:256], True, True))
+    w("s", m_d0)
+    kd0 = sig(S.activation(T.d0[:, :], ps[4][:, 0:256], F.Copy, scale=2048.0))
+    kso = sig(S.activation(cy(SO), cy(FO), F.Copy, scale=-1.0 / 32))
+    w("p", kr, kc)
+    mm(ps[2][:, 0:256], T.el[:, 0:128], T.er[:, 0:256], True, False)
+    mm(ps[2][:, 0:256], T.el[:, 128:256], T.er[:, 0:256], False, False)
+    mm(ps[2][:, 0:256], T.er[:, 0:128], T.ec[:, :], False, False)
+    mm(ps[0][:, 0:257], T.el[:, 256:384], T.er[:, 0:257], True, False)
+    tab1, tab2, kd, t_ost = new(), new(), new(), new()
+
+    def rows(tb, parts, a, b, ld, sm, src, tok):
+        landed("y", sm, src)
+        dsig(Y.dma_start(tb[parts, a:b], ld), tok)
+    w("y", c_pt, nm1)
+    for j, x in enumerate((T.nmb[:, 0:256], T.nmb[:, 256:512], T.pt[:, :])):
+        dsig(Y.dma_start(T.ost[j], x), t_ost)
 
     w("s", t_sc, c_nxt)
     w("v", t_sc, c_nxt)
@@ -261,174 +303,148 @@ def rank_program(g, core, T, topo):
         t = new()
         for hh in range(2):
             a = 1024 * j + 512 * hh
-            o, src = T.gat[:, a:a + 512], T.tab[:, :].indirect(T.nxt_u[:, a // 16:a // 16 + 32])
+            o, src = T.gat[:, 64 + a:64 + a + 512], T.tab[:, :].indirect(T.nxt_u[:, a // 16:a // 16 + 32])
             sig(S.activation(o, src, F.Copy) if hh else V.tensor_copy(o, src), t)
         gt.append(t)
-    m_cd = [new(), new()]
-    w("p", kr)
-    mm(ps[3][:, 0:256], T.t32[:, 0:128], T.t32[:, :], True, False)
-    mm(ps[3][:, 0:256], T.t32[:, 0:128], T.c32[:, :], False, False)
+    t_st = []
+    for hh in range(2):
+        w("y", gt[2 * hh], gt[2 * hh + 1])
+        t_st.append(dsig(Y.dma_start(T.st[hh], T.gat[0:128:8, 64 + 2048 * hh:2112 + 2048 * hh])))
+        w("g", t_st[hh])
+        send(d1, T.la1[hh], T.st[hh], "la1%d" % hh)
+        send(d2, T.la2[hh], T.st[hh], "la2%d" % hh)
+    ks = sig(iota(T.sl[:, :], [[16, 64]]))
+    sig(put(view(ZN, 15), 8, 1.0 / 256), k4)
+    sig(put(view(FN, RN), 5, 1.0), k4)
+    sig(put(view(FP, RS), 2, 1.0), k4)
+    sig(put(view(FR, RS), RS, 1.0), k4)
+    sig(put(view(FN, RS), 6, 1.0), k4)
+    w("g", kso)
+    sig(g.affine_select(cy(FT), cy(SO), [[1, 128]], A.is_ge, 0.0, 0, -1), k6)
+    sig(g.affine_select(cy(FS), cy(SO), [[-1, 128]], A.is_gt, 0.0, 0, 1), k6)
+    sig(iota(T.rw[:, :], [[16, 64]], 264, 1), k6)
+    w("y", t_ost)
+    for j in range(3):
+        dsig(Y.dma_start(T.dat[4 + j:128:16, 64:TW], T.ost[j]), tab1)
+    rows(T.dat, slice(2, 128, 16), 64, TW, T.lpt1[:, :], "lpt1_s", s1, tab1)
+    rows(T.dat, slice(RS, 128, 16), 64, TW, T.lpt3[:, :], "lpt3_s", s3, tab1)
+    for hh in range(2):
+        rows(T.dat, slice(0, 128, 8), 64 + 2048 * hh, 2112 + 2048 * hh, T.la1[hh], "la1%d" % hh, s1, tab1)
+
+    m_cd, t_nb, twq = [new(), new()], new(), new()
     w("p", kz)
     for j in range(4):
         w("p", gt[j])
         for kk in range(16):
-            m = mm(ps[6 + j // 2][:, 64 * (j % 2):64 * (j % 2) + 64], cz(ZN + 15 - kk),
-                   T.gat[:, 1024 * j + kk:1024 * j + 1024:16], kk == 0, kk == 15)
-        sig(m, m_cd[j // 2])
+            m = mm(ps[6 + j // 2][:, 64 * (j % 2):64 * (j % 2) + 64], T.zm[:, 128 * kk:128 * kk + 128],
+                   T.gat[:, 64 + 1024 * j + kk:64 + 1024 * j + 1024:16], kk == 0, kk == 15)
+        if j % 2:
+            sig(m, m_cd[j // 2])
+    w("y", m_cd[0], m_cd[1], *t_st)
+    rows(T.gat, slice(RS, 128, 16), 64, TW, T.lpt2[:, :], "lpt2_s", s2, tab2)
+    for hh in range(2):
+        rows(T.gat, slice(0, 128, 8), 64 + 2048 * hh, 2112 + 2048 * hh, T.la2[hh], "la2%d" % hh, s2, tab2)
+    cv = new()
+    for hh in range(2):
+        w("v", m_cd[hh])
+        sig(V.tensor_scalar(T.nb[:, 8 + 128 * hh:136 + 128 * hh], ps[6 + hh][:, 0:128], -1.0 / 32, 128.26, A.mult, A.add), t_nb)
+        w("s", t_nb)
+        sig(S.activation(T.wq[:, 128 * hh:128 * hh + 128], ps[6 + hh][:, 0:128], F.Identity, bias=-8.25), twq)
+        if not hh:
+            sig(S.activation(T.wn[:, 0:1024], T.zb[:, 0:1024], F.Identity, bias=30000.0), kd)
+            sig(V.tensor_scalar(T.colN[:, :], T.p16[:, :], -1.0, None, A.mult), cv)
+            sig(V.tensor_scalar(T.colF[:, :], T.p16[:, :], RN, -1.0, A.is_equal, A.mult), cv)
 
-    w("v", m_cd[0])
-    f_l, f_l0 = new(), new()
-    sig(V.tensor_scalar(T.fl[:, 8:136], ps[6][:, 0:128], 0.0, None, A.is_gt), f_l0)
-    hlc, x1, c_p5, nm1 = new(), new(), new(), new()
-    nm0 = sig(V.tensor_scalar(T.onh[:, :], T.own_i[:, :], 1.0 / 128, 128.0, A.mult, A.add))
-
-    def first(hh, fl_):
-        w("s", m_cd[hh], fl_)
-        x = sig(S.activation(T.hl[:, 128 * hh:128 * hh + 128], ps[6 + hh][:, 0:128], F.Identity, bias=B0, scale=1.0 / 1024), x1)
-        w("s", x)
-        sig(S.activation(T.p5[:, 128 * hh:128 * hh + 128], T.hl[:, 128 * hh:128 * hh + 128], F.Identity, bias=-1024.0 * B0,
-                         scale=1024.0), c_p5)
-
-    def second(hh):
-        w("v", c_p5)
-        sig(V.tensor_tensor(T.hl[:, 256 + 128 * hh:384 + 128 * hh], ps[6 + hh][:, 0:128], T.p5[:, 128 * hh:128 * hh + 128],
-                            A.subtract), hlc)
-    first(0, f_l0)
-    second(0)
-    w("s", nm0)
-    n128 = sig(S.activation(ps[1][:, 0:256], T.onh[:, :], F.Identity, bias=-16384.0, scale=128.0))
-    w("v", m_cd[1])
-    sig(V.tensor_scalar(T.fl[:, 136:264], ps[7][:, 0:128], 0.0, None, A.is_gt), f_l)
-    w("v", k3)
-    z1h = sig(V.tensor_copy(T.z1[:, :], cz(Z1, 144)))
-    first(1, f_l)
-    sig(S.activation(T.nmb[:, 0:256], T.onh[:, :], F.Identity, bias=-128.0), nm1)
-    w("p", f_l0, f_l, zz, c_pt, kf, k3, k4)
-    m_c = sig(mm(ps[2][:, 0:257], cz(FO), T.fl[:, 7:264], True, True))
-    m_x = sig(mm(ps[3][:, 0:256], cz(ON4), T.fl[:, 8:264], False, True))
-    w("v", m_c, z0)
-    ta = sig(V.tensor_tensor_scan(T.ax[:, :], ps[2][:, 0:257], T.zb[:, 0:257], 0.0, A.add, A.add))
+    w("p", t_nb, zz)
+    m_c = sig(mm(ps[0][:, 0:257], cy(SL), T.nb[:, 7:264], False, True))
+    m_x = sig(mm(ps[2][:, 0:256], cy(ON4), T.nb[:, 8:264], False, True))
+    w("v", kx)
+    zxh = sig(V.tensor_copy(T.zx[:, :], cz(ZX, 288)))
+    t_mk = sig(S.activation(T.mk[:, 0:1024], T.zb[:, 0:1024], F.Silu))
+    w("v", m_c)
+    ta = sig(V.tensor_tensor_scan(T.ax[:, :], ps[0][:, 0:257], T.zb[:, 0:257], 0.0, A.add, A.add))
     w("v", ta, m_x)
-    to = sig(V.tensor_tensor(T.o16[:, :], T.ax[:, 0:256], ps[3][:, 0:256], A.max))
-    second(1)
-    w("p", z1h, to)
-    for k in range(16):
-        m = mm(ps[5][:, 0:16], T.z1[:, 15 - k:143 - k], T.o16[:, k:256:16], k == 0, k == 15)
-    m_o = sig(m)
-    mm(ps[4][:, 0:256], cz(FT), T.fl[:, 8:264], True, False)
-    m_p = sig(mm(ps[4][:, 0:256], cz(DG), T.fl[:, 8:264], False, True))
-    w("p", x1, hlc)
-    mm(ps[0][:, 0:256], cz(I256), T.hl[:, 0:256], True, False)
-    m_cp = sig(mm(ps[0][:, 0:256], cz(I1), T.hl[:, 256:512], False, True))
-    w("s", m_cp)
-    tcd = sig(S.activation(T.cd[:, :], ps[0][:, 0:256], F.Identity, bias=-2304.0 - BW))
-    w("g", x1, hlc)
-    send(d1, T.lhl1[:, :], T.hl[:, :], "lhl1_s")
-    send(d2, T.lhl2[:, :], T.hl[:, :], "lhl2_s")
-    cu = new()
-    sig(V.tensor_scalar(T.colU[:, :], T.p16[:, :], 256.0, None, A.mult), cu)
-    w("v", n128)
-    sig(V.tensor_tensor(T.nmb[:, 256:512], T.own_i[:, :], ps[1][:, 0:256], A.subtract), nm1)
-    w("s", nm1, t_sc)
-    dsig(S.dma_start(T.dat[4:128:16, :], T.nmb[:, 0:256]), tab0)
-    dsig(S.dma_start(T.dat[5:128:16, :], T.nmb[:, 256:512]), tab0)
-    w("v", m_o)
-    tol = sig(V.tensor_copy(T.ol[:, :], ps[5][:, 0:16]))
-    w("v", tol, t_mk, k5)
-    tmk = sig(V.tensor_copy(T.mk[:, :].indirect(T.ol[:, :]), T.cio[:, :]))
+    t = sig(V.tensor_tensor(T.oy[:, :], T.ax[:, 0:256], ps[2][:, 0:256], A.max))
+    w("v", t, kd0)
+    t = sig(V.tensor_tensor_scan(T.oh[:, :], T.d0[:, :], T.oy[:, :], 0.0, A.add, A.min))
+    w("v", t)
+    tol = sig(V.tensor_copy(T.ol[:, :], T.oh[:, 15:256:16]))
+    w("v", tol, twq, kd)
+    t = sig(V.tensor_copy(T.wn[:, :].indirect(T.ol[:, :]), T.wq[:, :]))
+    w("v", t, kc32)
+    t = sig(V.tensor_tensor_scan(T.dd[:, :], T.wn[:, 0:1024], T.c32[:, :], 100.0, A.min, A.add))
+    w("v", t)
+    tdc = sig(V.tensor_scalar(T.dc[:, :], T.dd[:, :], -8.0, 8.0, A.max, A.min))
+    w("p", tdc, zxh, nm1)
+    m_l2 = fold(ps[5][:, 0:64], T.zx, 0, T.dc)
+    w("s", tol, t_mk, kcf)
+    tmk = sig(S.activation(T.mk[:, :].indirect(T.ol[:, :]), T.cf[:, :], F.Silu))
     w("v", tmk)
-    tcm = sig(V.tensor_tensor_scan(T.cm[:, :], T.mk[:, 0:1024], T.zb[:, 0:1024], 0.0, A.max, A.max))
-    w("p", tcm)
-    for k in range(16):
-        m = mm(ps[5][:, 64:128], cz(Z1 + 15 - k), T.cm[:, k:1024:16], k == 0, k == 15)
-    m_l1 = sig(m)
-    for k in range(16):
-        mm(ps[2][:, 0:64], cz(Z1 + 15 - k), T.cm[:, k:1024:16], k == 0, False)
-    w("v", m_p)
-    twq = sig(V.tensor_tensor(T.wq[:, :], T.ax[:, 0:256], ps[4][:, 0:256], A.add))
-    w("v", k4)
-    zxh = sig(V.tensor_copy(T.zx[:, :], cz(ZX, 144)))
-    w("v", m_l1)
-    tl1 = sig(V.tensor_copy(T.l1[:, :], ps[5][:, 64:128]))
-    w("v", tl1, twq, km)
-    tse = sig(V.tensor_tensor(T.sel[:, :], T.wq[:, :].indirect(T.l1[:, :]), T.mrow[:, :], A.is_equal))
-    for tb, ld, sm, src, tok in ((T.tb1, T.lhl1, "lhl1_s", s1, tab1), (T.tb2, T.lhl2, "lhl2_s", s2, tab2)):
-        landed("y", sm, src)
-        for s_ in range(2):
-            dsig(Y.dma_start(tb[s_:128:16, 16:4112], ld[:, 256 * s_:256 * s_ + 256]), tok)
-
-    w("s", k4, cu)
-    ksc, fw, ttm, cv = new(), new(), new(), new()
-    sig(S.activation(view(ZU, 15), vx, F.Copy, scale=T.colU[:, :]), ksc)
-    w("p", tse, ksc)
-    for k in range(16):
-        m = mm(ps[2][:, 0:64], cz(ZU + 15 - k), T.sel[:, k:1024:16], False, k == 15)
-    m_lo = sig(m)
-    w("v", tse, tcd)
-    ths = sig(V.tensor_tensor(T.hls[:, :], T.cd[:, :].indirect(T.l1[:, :]), T.sel[:, :], A.mult))
-    w("p", ths, zxh)
-    for k in range(16):
-        m = mm(ps[5][:, 128:192], T.zx[:, 15 - k:143 - k], T.hls[:, k:1024:16], k == 0, k == 15)
-    m_l2 = sig(m)
-    tll0, tll = new(), new()
-    w("v", m_lo)
-    sig(V.tensor_copy(T.ll[:, 64:128], ps[2][:, 0:64]), tll0)
-    sig(V.tensor_scalar(T.colN[:, :], T.p16[:, :], -1.0, None, A.mult), cv)
-    sig(V.tensor_scalar(T.colF[:, :], T.p16[:, :], 8, -1.0, A.is_equal, A.mult), cv)
-
-    def pick(q, tb, lst, at, u, v, out, tok, *toks):
-        w(q, *toks)
-        src, o = tb[:, :].indirect(lst[:, at + u:at + v]), out[:, 16 * u:16 * v]
-        sig(V.tensor_copy(o, src) if q == "v" else S.activation(o, src, F.Copy), tok)
-    tng, tr1, tr2 = new(), new(), new()
-    pick("s", T.dat, T.ll, 64, 0, N0, T.ng, tng, tll0, tab0)
-    w("v", m_l2)
-    sig(V.tensor_scalar(T.ll[:, 0:64], ps[5][:, 128:192], 2063.0, None, A.add), tll)
-    pick("v", T.tb1, T.ll, 0, 0, R1, T.r1, tr1, tll, tab1)
-    pick("s", T.tb1, T.ll, 0, R1, 64, T.r1, tr1, tll, tab1)
-    pick("v", T.dat, T.ll, 64, N0, N1, T.ng, tng, tll0, tab0)
-    pick("s", T.dat, T.ll, 64, N1, 64, T.ng, tng, tll0, tab0)
-    w("p", tcd, nm1, tll, tr1)
-    for k in range(16):
-        m = mm(ps[1][:, 0:64], cz(ZW + 15 - k), T.r1[:, k:1024:16], k == 0, k == 15)
-    m_l3 = sig(m)
-    w("p", hlc, tng)
-    mm(ps[6][:, :], cz(FN), T.ng[:, 0:512], True, False)
-    m_ac = sig(mm(ps[6][:, :], cz(FP), T.r1[:, 0:512], False, True))
+    tcm = sig(V.tensor_tensor_scan(T.cm[:, :], T.mk[:, 0:1024], T.mk[:, 0:1024], CB, A.max, A.max))
+    fw, ttm, kq = new(), new(), new()
     w("s", ta, cv)
     sig(S.activation(T.totm[:, :], T.ax[:, 256:257], F.Identity, bias=T.colN[:, :]), ttm)
+    sig(S.activation(cy(IC), cy(I4), F.Copy, scale=1024.0), kq)
     sig(S.activation(T.win[:, 0:264], T.zb[:, 0:264], F.Identity, bias=T.colF[:, :]), fw)
-    w("v", m_l3)
-    tl3 = sig(V.tensor_scalar(T.l3[:, :], ps[1][:, 0:64], -241.0 - BW, None, A.add))
-    pick("v", T.tb2, T.l3, 0, 0, R2, T.r2, tr2, tl3, tab2)
-    pick("s", T.tb2, T.l3, 0, R2, 64, T.r2, tr2, tl3, tab2)
+    w("v", m_l2)
+    txi = sig(V.tensor_scalar(T.xi[:, :], ps[5][:, 0:64], 32768.0, None, A.add))
     w("v", ttm, ks)
     ttk = sig(V.tensor_scalar(T.tk[:, :], T.sl[:, :], T.totm[:, :], None, A.is_ge))
+    w("v", txi)
+    txp = sig(V.tensor_scalar(T.xp[:, :], T.xi[:, :], 4095, None, A.bitwise_and))
+    w("s", txi)
+    tpb = sig(S.activation(T.pb[:, :], ps[5][:, 0:64], F.Identity, bias=136.5001, scale=1.0 / 4096))
+    w("v", txp)
+    tll = sig(V.tensor_copy(T.ll[:, 0:64], T.xp[:, :]))
+
+    def pick(q, win, lst, at_, u, v, out, tok, *toks):
+        w(q, *toks)
+        src, o = win.indirect(lst[:, at_ + u:at_ + v]), out[:, 16 * u:16 * v]
+        sig(V.tensor_copy(o, src) if q == "v" else S.activation(o, src, F.Copy), tok)
+    tng, tr1, tr2 = [new(), new()], new(), new()
+    pick("v", T.dat[:, 64:TW], T.ll, 0, 0, R1, T.r1, tr1, tll, tab1)
+    pick("s", T.dat[:, 64:TW], T.ll, 0, R1, 64, T.r1, tr1, tll, tab1)
+    w("p", tcm, kq)
+    fold(ps[3][:, 0:64], T.zx, 144, T.cm, False)
+    w("p", tpb)
+    m_lo = sig(mm(ps[3][:, 0:64], cy(IC), T.pb[:, :], False, True))
+    w("p", tr1, ta, k4)
+    m_l3 = fold(ps[0][:, 0:64], T.cz, ZN, T.r1)
+    w("v", m_lo)
+    tll0 = sig(V.tensor_scalar(T.ll[:, 64:128], ps[3][:, 0:64], -129.0 * 256 - CB, 4095.0, A.add, A.min))
     w("s", ttk)
-    tth = sig(S.activation(T.thr[:, :], T.tk[:, :], F.Copy, bias=BW, scale=8192.0))
+    tth = sig(S.activation(T.thr[:, :], T.tk[:, :], F.Copy, scale=64.0))
+    pick("v", T.dat[:, 64:TW], T.ll, 64, 0, N1, T.ng, tng[0], tll0)
+    pick("s", T.dat[:, 64:TW], T.ll, 64, N1, 64, T.ng, tng[1], tll0)
+    w("v", m_l3)
+    tl3 = sig(V.tensor_scalar(T.l3[:, :], ps[0][:, 0:64], 256.0, None, A.mult))
+    pick("v", T.gat[:, :], T.l3, 0, 0, R2, T.r2, tr2, tl3, tab2, zz)
+    pick("s", T.gat[:, :], T.l3, 0, R2, 64, T.r2, tr2, tl3, tab2, zz)
+    w("p", twq)
+    mm(ps[6][:, :], cz(FP), T.r1[:, 0:512], True, False)
+    mm(ps[7][:, :], cz(FP), T.r1[:, 512:1024], True, False)
+    w("p", tng[0], tng[1])
+    m_ac = sig(mm(ps[6][:, :], cz(FN), T.ng[:, 0:512], False, True))
+    mm(ps[7][:, :], cz(FN), T.ng[:, 512:1024], False, False)
     w("p", tr2)
-    for k in range(16):
-        m = mm(ps[0][:, 256:320], cz(ZW + 15 - k), T.r2[:, k:1024:16], k == 0, k == 15)
-    m_l4 = sig(m)
+    m_l4 = fold(ps[1][:, 0:64], T.cz, ZN, T.r2)
+    m_ad = sig(mm(ps[7][:, :], cz(FR), T.r2[:, 512:1024], False, True))
     w("v", m_ac, tr2)
     tfd = [sig(V.tensor_tensor(T.fd[:, 0:512], ps[6][:, :], T.r2[:, 0:512], A.add))]
 
     w("v", m_l4)
-    tl5 = sig(V.tensor_scalar(T.l5[:, :], ps[0][:, 256:320], -241.0 - BW, None, A.add))
+    tl5 = sig(V.tensor_scalar(T.l5[:, :], ps[1][:, 0:64], 256.0, None, A.mult))
     w("v", tth)
-    f4 = sig(V.tensor_tensor(T.fl4[:, 8:72], ps[0][:, 256:320], T.thr[:, :], A.is_gt))
-    x2 = sig(V.tensor_tensor(T.xn[:, :], ps[0][:, 256:320], T.thr[:, :], A.is_le))
-    w("s", tl5)
-    tr3 = [sig(S.activation(T.r3[:, 512 * hh:512 * hh + 512], T.tb1[:, :].indirect(T.l5[:, 32 * hh:32 * hh + 32]), F.Copy))
-           for hh in range(2)]
-    mm(ps[7][:, :], cz(FN), T.ng[:, 512:1024], True, False)
-    w("p", f4, zz)
-    mm(ps[2][:, 0:64], cz(FS), T.fl4[:, 7:71], True, False)
-    m_a = sig(mm(ps[2][:, 0:64], cz(FT), T.fl4[:, 8:72], False, True))
-    mm(ps[7][:, :], cz(FP), T.r1[:, 512:1024], False, False)
-    m_ad = sig(mm(ps[7][:, :], cz(FR), T.r2[:, 512:1024], False, True))
+    f4 = sig(V.tensor_tensor(T.fl4[:, 8:72], ps[1][:, 0:64], T.thr[:, :], A.is_gt))
+    x2 = sig(V.tensor_tensor(T.xn[:, :], ps[1][:, 0:64], T.thr[:, :], A.is_le))
+    w("s", tl5, zz)
+    tr3 = [sig(S.activation(T.r3[:, 0:512], T.dat[:, :].indirect(T.l5[:, 0:32]), F.Copy))]
+    w("p", f4, zz, tol, k6)
+    mm(ps[2][:, 0:64], cy(FS), T.fl4[:, 7:71], True, False)
+    m_a = sig(mm(ps[2][:, 0:64], cy(FT), T.fl4[:, 8:72], False, True))
     w("s", m_ad)
     tfd.append(sig(S.activation(T.fd[:, 512:1024], ps[7][:, :], F.Copy)))
+    tr3.append(sig(S.activation(T.r3[:, 512:1024], T.dat[:, :].indirect(T.l5[:, 32:64]), F.Copy)))
     w("v", x2, k6)
     x3 = sig(V.tensor_tensor(T.xx[:, :], T.xn[:, :], T.rw[:, :], A.mult))
     w("v", m_a)
@@ -448,8 +464,8 @@ def rank_program(g, core, T, topo):
     w("y", tw)
     t_y = new()
     w("s", tw)
-    dsig(Y.dma_start(T.yk[:, :], T.win[8:128:16, 1:257]), t_y)
-    dsig(S.dma_start(T.ys[:, :], T.win[9:128:16, 1:257]), t_y)
+    dsig(Y.dma_start(T.yk[:, :], T.win[RN:128:16, 1:257]), t_y)
+    dsig(S.dma_start(T.ys[:, :], T.win[RS:128:16, 1:257]), t_y)
     for t in made:
         if waited.get(t[0], 0) < t[1]:
             w("y", t)

@@ -1,3 +1,4 @@
+from concourse.bass import DstId, RemoteDMATransfer
 from concourse.mybir import AluOpType as A, ActivationFunctionType as F
 
 BF, F32, F16, I32, U16 = "bfloat16", "float32", "float16", "int32", "uint16"
@@ -5,47 +6,55 @@ TW = 4160
 SCRATCH = {
     "own_i": ("sbuf", [128, 256], I32), "nxt_i": ("sbuf", [128, 256], I32), "pts_i": ("sbuf", [128, 256], I32),
     "own_u": ("sbuf", [128, 256], U16), "nxt_u": ("sbuf", [128, 256], U16), "own_r": ("sbuf", [128, 256], U16),
-    "nf": ("sbuf", [128, 256], F32), "onh": ("sbuf", [128, 256], BF), "nmb": ("sbuf", [128, 512], BF),
+    "nf": ("sbuf", [128, 256], F32), "onh": ("sbuf", [128, 256], BF), "nmb": ("sbuf", [128, 256], BF),
     "ptsb": ("sbuf", [128, 256], BF), "zb": ("sbuf", [128, 1040], BF),
     "tab": ("sbuf", [128, 16384], BF), "dat": ("sbuf", [128, TW], BF), "gat": ("sbuf", [128, TW], BF),
     "pidx": ("sbuf", [128, 1], I32), "p16": ("sbuf", [128, 1], I32),
     "colA": ("sbuf", [128, 1], F32), "colB": ("sbuf", [128, 1], F32), "colC": ("sbuf", [128, 1], F32),
-    "colF": ("sbuf", [128, 1], F32), "colN": ("sbuf", [128, 1], F32), "totm": ("sbuf", [128, 1], F32),
+    "colF": ("sbuf", [128, 1], F32), "colI": ("sbuf", [128, 1], F32),
     "io64": ("sbuf", [128, 64], BF), "lb": ("sbuf", [128, 64], F32),
-    "cz": ("sbuf", [128, 816], BF), "cy": ("sbuf", [128, 1536], BF), "i32": ("sbuf", [128, 128], F32),
-    "zm": ("sbuf", [128, 2048], BF), "ep": ("sbuf", [8, 144], BF), "zx": ("sbuf", [128, 288], F16),
-    "er": ("sbuf", [16, 272], BF), "ec": ("sbuf", [16, 256], BF), "el": ("sbuf", [16, 384], BF),
+    "cz": ("sbuf", [128, 688], BF), "cy": ("sbuf", [128, 1792], BF), "i32": ("sbuf", [128, 128], F32),
+    "zm": ("sbuf", [128, 2048], BF), "ep": ("sbuf", [8, 144], BF), "zx": ("sbuf", [128, 144], F16),
+    "er": ("sbuf", [16, 256], BF), "ec": ("sbuf", [16, 256], BF), "el": ("sbuf", [16, 384], BF),
     "d0": ("sbuf", [128, 256], BF), "c32": ("sbuf", [128, 1024], BF),
-    "cio": ("sbuf", [16, 256], BF), "cf": ("sbuf", [128, 256], F32), "rw": ("sbuf", [128, 64], F32),
-    "sl": ("sbuf", [128, 64], F32), "tk": ("sbuf", [128, 64], F32), "thr": ("sbuf", [128, 64], F32),
+    "cio": ("sbuf", [16, 256], BF), "cf": ("sbuf", [128, 256], F32), "yt": ("sbuf", [128, 64], F32),
     "mk": ("sbuf", [128, 1280], F32), "wn": ("sbuf", [128, 1280], F32),
     "pr8": ("sbuf", [8, 4096], BF), "pt": ("sbuf", [128, 256], BF),
     "ng": ("sbuf", [128, 1024], BF), "nb": ("sbuf", [128, 272], BF),
     "ax": ("sbuf", [128, 257], F32), "oy": ("sbuf", [128, 256], F16), "oh": ("sbuf", [128, 256], F16),
-    "wq": ("sbuf", [128, 256], F32), "ol": ("sbuf", [128, 16], U16), "cm": ("sbuf", [128, 1024], F16),
+    "wq": ("sbuf", [128, 256], F32), "ol": ("sbuf", [128, 16], U16), "cm": ("sbuf", [128, 1024], BF),
+    "mb": ("sbuf", [128, 1024], BF),
     "dd": ("sbuf", [128, 1024], F16), "dc": ("sbuf", [128, 1024], F16),
-    "xi": ("sbuf", [128, 64], I32), "xp": ("sbuf", [128, 64], I32), "pb": ("sbuf", [128, 64], BF),
+    "tk": ("sbuf", [128, 64], BF), "pb": ("sbuf", [128, 64], BF),
     "ll": ("sbuf", [128, 128], U16), "l3": ("sbuf", [128, 64], U16), "l4": ("sbuf", [128, 64], U16),
     "l5": ("sbuf", [128, 64], U16),
     "r1": ("sbuf", [128, 1024], BF), "r2": ("sbuf", [128, 1024], BF), "r3": ("sbuf", [128, 1024], F32),
-    "fl4": ("sbuf", [128, 72], BF), "xn": ("sbuf", [128, 64], F32), "xx": ("sbuf", [128, 64], F32),
-    "a4": ("sbuf", [128, 64], F32), "o4": ("sbuf", [128, 64], F32),
-    "fd": ("sbuf", [128, 1024], F32), "win": ("sbuf", [128, 1408], F32),
+    "fl4": ("sbuf", [128, 72], BF), "yb": ("sbuf", [128, 72], F16),
+    "ih": ("sbuf", [128, 256], F16), "y0": ("sbuf", [128, 64], F32), "a4": ("sbuf", [128, 64], F32),
+    "fd": ("sbuf", [128, 1024], F32), "win": ("sbuf", [128, 2688], F32),
     "lpt1": ("dram", [128, 256], BF), "lpt2": ("dram", [128, 256], BF), "lpt3": ("dram", [128, 256], BF),
-    "pst": ("dram", [128, 256], BF), "ost": ("dram", [3, 128, 256], BF), "st": ("dram", [2, 128, 256], BF), "la1": ("dram", [2, 128, 256], BF), "la2": ("dram", [2, 128, 256], BF),
+    "pst": ("dram", [128, 256], BF), "ost": ("dram", [3, 128, 256], BF),
 }
 for _b in range(8):
     SCRATCH["ps%d" % _b] = ("psum", [128, 512], F32)
-NE = 138
-SEMAPHORES = ["own_r_s", "lpt1_s", "lpt2_s", "lpt3_s", "la10", "la11", "la20", "la21", "ls"] + ["e%d" % _i for _i in range(NE)]
+PIECES = ((0, 2), (2, 3), (3, 4))
+for _k, (_a, _b) in enumerate(PIECES):
+    for _nm in ("st", "la1", "la2"):
+        SCRATCH["%s%d" % (_nm, _k)] = ("dram", [128, 128 * (_b - _a)], BF)
+NE = 130
+SEMAPHORES = (["own0_s", "own_r_s", "lpt_s", "ls"] + ["e%d" % _i for _i in range(NE)]
+              + ["la%d%d_s" % (_d, _k) for _d in (1, 2) for _k in range(len(PIECES))])
 
-ZN, ZX, Z1, FN, FP, FR = 0, 144, 288, 432, 560, 688
+ZN, ZX, Z1, FN, FP = 0, 144, 288, 432, 560
+XB = 3 * 262144.0 - 32768
 CB = 32.0
-I4, IL, FO, WT, SO, WL, FT, FS, SL, ON4, IB, IC = (128 * _k for _k in range(12))
-TG0, TG, TD, TS = 640, 1792, 3072, 5632
-VA = (768, 768, 512)
+I4, IL, FO, WT, WS, FT, FS, SL, SF, ON4, SG, IB, IC, IM = (128 * _k for _k in range(14))
+TG0, TG, TD, TS = 704, 1344, 5376, 5056
+VA = (768, 512, 512, 256)
 AE = 1536
-N1, R1, R2 = 24, 36, 36
+MK, PA = 896, 20
+FA, FB = 512, 832
+N1, R1, R2 = 28, 32, 32
 RN, RS, RF = 10, 9, 12
 
 
@@ -104,9 +113,9 @@ def rank_program(g, core, T, topo):
     def mm(out, lhsT, rhs, first, last):
         return P.matmul(out, lhsT, rhs, first, last)
 
-    def fold(out, mat, at_, rows_, last=True):
+    def fold(out, mat, at_, rows_, last=True, first=True):
         for k in range(16):
-            m = mm(out, mat[:, at_ + 15 - k:at_ + 143 - k], rows_[:, k:1024:16], k == 0, last and k == 15)
+            m = mm(out, mat[:, at_ + 15 - k:at_ + 143 - k], rows_[:, k:1024:16], first and k == 0, last and k == 15)
         return sig(m) if last else None
 
     ps = [T["ps%d" % b] for b in range(8)]
@@ -151,8 +160,9 @@ def rank_program(g, core, T, topo):
     zeros(VA[1])
     w("v", cc)
     c2 = sig(V.tensor_scalar(T.colC[:, :], T.p16[:, :], RF, T.colA[:, :], A.is_equal, A.add))
+    zeros(VA[3])
     w("v", t_own)
-    c_own = sig(V.tensor_copy(T.own_u[:, :], T.own_i[:, :]))
+    c_own = [sig(V.tensor_copy(T.own_u[:, a:b], T.own_i[:, a:b])) for a, b in ((0, AE // 16), (AE // 16, 256))]
     w("v", c2)
     b1 = sig(V.tensor_scalar(T.lb[:, :], T.io64[:, :], T.colA[:, :], None, A.mult))
     da = sig(V.tensor_scalar(T.dat[:, 64:128], T.io64[:, :], T.colB[:, :], T.colC[:, :], A.mult, A.add))
@@ -170,12 +180,13 @@ def rank_program(g, core, T, topo):
     w("v", t_pts)
     c_pts = sig(V.tensor_copy(T.ptsb[:, :], T.pts_i[:, :]))
     double(256, 0, 256)
-    w("v", t_nxt)
-    c_nxt = sig(V.tensor_copy(T.nxt_u[:, :], T.nxt_i[:, :]))
+    zeros(512)
     double(512, 0, 512)
     zeros(512)
     double(1024, 0, AE - 1024)
     zeros(16384 - at[0])
+    w("v", t_nxt)
+    c_nxt = sig(V.tensor_copy(T.nxt_u[:, :], T.nxt_i[:, :]))
     db = new()
     w("s", b1, da)
     for to, frm, width in ((AE, AE - 1024, 2048 - AE), (2048, 0, 1024), (3072, 0, 1024)):
@@ -183,25 +194,28 @@ def rank_program(g, core, T, topo):
         sig(S.activation(T.dat[:, 64 + to:64 + to + width], T.dat[:, 64 + frm:64 + frm + width], F.Identity,
                          bias=T.lb[:, k:k + 1]), db)
 
-    w("g", c_own)
-    send(d1, T.own_r[:, :], T.own_u[:, :], "own_r_s")
+    w("g", c_own[0])
+    send(d1, T.own_r[:, 0:AE // 16], T.own_u[:, 0:AE // 16], "own0_s")
+    w("g", c_own[1])
+    send(d1, T.own_r[:, AE // 16:256], T.own_u[:, AE // 16:256], "own_r_s")
     sig(iota(T.tab[:, TG0:TG], [[0, TG - TG0]]), f_tab)
 
     w("v", f_tab, f_tabv, t_tab, da)
-    landed("v", "own_r_s", s1)
+    landed("v", "own0_s", s1)
     t_s0 = sig(V.tensor_copy(T.tab[:, :].indirect(T.own_r[:, 0:AE // 16]), T.dat[:, 64:64 + AE]))
+    landed("v", "own_r_s", s1)
     w("v", db, t_s0)
     t_sc = sig(V.tensor_copy(T.tab[:, :].indirect(T.own_r[:, AE // 16:256]), T.dat[:, 64 + AE:TW]))
 
     w("y", c_pts)
+    landed("y", "own0_s", s1)
     t_pst = dsig(Y.dma_start(T.pst[:, :], T.ptsb[:, :]))
-    w("y", t_pst)
-    t_pr8 = dsig(Y.dma_start(T.pr8[:, :], T.pst[:, :]))
     landed("y", "own_r_s", s1)
+    t_pr8 = dsig(Y.dma_start(T.pr8[:, :], T.ptsb[:, :]))
     t_zm = new()
     for a in (0, 1024):
         dsig(Y.dma_start(T.zm[:, a:a + 1024], T.zb[:, 0:1024]), t_zm)
-    t_cz = dsig(Y.dma_start(T.cz[:, :], T.zb[:, 0:816]))
+    t_cz = dsig(Y.dma_start(T.cz[:, :], T.zb[:, 0:688]))
 
     def view(b, start):
         return T.cz[:, b + start:b + start + 113:16]
@@ -225,23 +239,26 @@ def rank_program(g, core, T, topo):
     kt = sig(g.affine_select(cy(WT), cy(FO), [[1, 128]], A.is_ge, 0.0, 0, -1))
     k2 = sig(g.affine_select(T.ep[:, :], T.zb[0:8, 0:144], [[1, 144]], A.not_equal, 1.0, -15, -16))
     w("g", t_pst)
-    send(d1, T.lpt1[:, :], T.pst[:, :], "lpt1_s")
-    send(d2, T.lpt2[:, :], T.pst[:, :], "lpt2_s")
-    send(d3, T.lpt3[:, :], T.pst[:, :], "lpt3_s")
-    kl = sig(g.affine_select(cy(WL), cy(FO), grp, A.is_equal, 0.0, 15, -1))
+    eng = [e for e in topo.engines(core, d1) if e in topo.engines(core, d2) and e in topo.engines(core, d3)]
+    g.remote_dma_fused([RemoteDMATransfer(dst_ids=[DstId(rid=topo.addr(d)[0], pnc=topo.addr(d)[1]) for d in (d1, d3, d2)],
+                                          dma_engine_mask=sum(1 << e for e in eng), remote_sem=T.sem.lpt_s, src=T.pst[:, :],
+                                          dsts=[T.lpt1[:, :], T.lpt3[:, :], T.lpt2[:, :]])], local_sem=T.sem.ls)
+    ls[0] += len(eng)
+    kl = sig(g.affine_select(cy(SL), z128, grp, A.not_equal, 1.0, 15, -1))
+    sig(g.affine_select(cy(SF), z128, grp, A.not_equal, 1.0, RF, -1), kl)
+    ke = sig(g.affine_select(T.er[:, :], T.zb[0:16, 0:256], [[0, 16], [1, 16]], A.not_equal, 1.0, 0, -1))
     k5 = sig(iota(T.cio[:, :], [[1, 256]]))
-    ke = sig(g.affine_select(T.er[:, :], T.zb[0:16, 0:272], [[0, 17], [1, 16]], A.not_equal, 1.0, 0, -1))
     w("g", k5)
     kc = sig(g.affine_select(T.ec[:, :], T.cio[:, :], [[0, 16], [1, 16]], A.is_equal, 0.0, 0, -1))
+    kc0 = sig(iota(T.c32[:, 0:256], [[0, 256]], 32))
     w("g", t_cz)
     sig(setw(vx, vx, [[16, 8]], 256.0, -1, -1), k3)
-    sig(put(view(ZN, 15), 0, 0.25), k3)
-    sig(put(view(FN, RN), 4, 128.0), k3)
-    kx = sig(put(view(Z1, 15), 0, 1.0))
-    w("g", k3)
-    sig(setw(vx, vx, [[16, 8]], 0.0, 15, -1), kx)
     kcf = sig(iota(T.cf[:, :], [[1, 256]], int(CB)))
-    kc32 = sig(iota(T.c32[:, :], [[0, 1024]], 32))
+    w("g", k3)
+    kx = sig(setw(vx, vx, [[16, 8]], 0.0, 15, -1))
+    t_mk = sig(iota(T.mk[:, 0:MK], [[0, MK]]))
+    sig(g.affine_select(cy(WS), cy(FO), [[-1, 128]], A.is_gt, 0.0, 0, 1), k6)
+    sig(iota(T.y0[:, :], [[32, 64]], 32), k6)
     w("y", t_zm, ki, kt)
     for part, b in ((0, I4), (8, IL), (RF, WT)):
         dsig(Y.dma_start(T.zm[part:128:16, :], cy(b)), kz)
@@ -258,43 +275,45 @@ def rank_program(g, core, T, topo):
     sig(S.activation(T.i32[:, :], cy(I4), F.Copy, scale=-128.0), kb)
     sig(S.activation(cy(IB), cy(I4), F.Copy, scale=16384.0), kb)
     sig(S.activation(T.nb[:, 0:8], T.zb[:, 0:8], F.Identity, bias=128.0), zz)
-    sig(S.activation(T.fl4[:, 0:8], T.zb[:, 0:8], F.Copy), zz)
-    sig(S.activation(T.dat[:, 0:64], T.zb[:, 0:64], F.Copy), zz)
-    sig(S.activation(T.gat[:, 0:64], T.zb[:, 0:64], F.Copy), zz)
-    w("s", nm0)
-    sig(S.activation(T.nmb[:, 0:256], T.onh[:, :], F.Identity, bias=-128.0), nm1)
     sig(S.activation(T.el[:, 128:256], T.zb[0:16, 0:128], F.Identity, bias=262144.0), kr)
     sig(S.activation(T.el[:, 256:384], T.zb[0:16, 0:128], F.Identity, bias=-128.0), kr)
+    kw0 = sig(S.activation(T.wn[:, 0:512], T.zb[:, 0:512], F.Identity, bias=30000.0))
     w("s", m_pt)
     c_pt = sig(S.activation(T.pt[:, :], ps[4][:, 0:256], F.Copy))
     w("p", kb, nm0, c_nf)
     mm(ps[5][:, 0:256], T.i32[:, :], T.nf[:, :], True, False)
     m_nl = sig(mm(ps[5][:, 0:256], cy(IB), T.onh[:, :], False, True))
     w("s", kl)
-    sig(S.activation(cy(ON4), cy(WL), F.Copy, scale=64.0), kr)
-    sig(S.activation(cy(SL), cy(WL), F.Copy, scale=-1.0 / 32), kr)
+    sig(S.activation(T.cy[:, ON4:ON4 + 256], T.cy[:, SL:SL + 256], F.Copy, scale=-2048.0), kr)
     w("s", m_nl)
-    sig(S.activation(T.nmb[:, 256:512], ps[5][:, 0:256], F.Identity, bias=16384.0, scale=-1.0 / 32), nm1)
+    sig(S.activation(T.nmb[:, :], ps[5][:, 0:256], F.Identity, bias=16384.0, scale=-1.0 / 32), nm1)
     w("s", ke)
     sig(S.activation(T.el[:, 0:128], T.er[:, 0:128], F.Identity, bias=41984.0, scale=-40960.0), kr)
     w("p", c_pt, ke)
     m_d0 = sig(mm(ps[4][:, 0:256], T.er[:, 0:128], T.er[:, 0:256], True, True))
     w("s", m_d0)
     kd0 = sig(S.activation(T.d0[:, :], ps[4][:, 0:256], F.Copy, scale=2048.0))
-    kso = sig(S.activation(cy(SO), cy(FO), F.Copy, scale=-1.0 / 32))
     w("p", kr, kc)
-    mm(ps[2][:, 0:256], T.el[:, 0:128], T.er[:, 0:256], True, False)
-    mm(ps[2][:, 0:256], T.el[:, 128:256], T.er[:, 0:256], False, False)
-    mm(ps[2][:, 0:256], T.er[:, 0:128], T.ec[:, :], False, False)
-    mm(ps[0][:, 0:257], T.el[:, 256:384], T.er[:, 0:257], True, False)
+    mm(ps[2][:, 0:192], T.el[:, 0:128], T.er[:, 0:192], True, False)
+    mm(ps[2][:, 0:192], T.el[:, 128:256], T.er[:, 0:192], False, False)
+    mm(ps[2][:, 0:192], T.er[:, 0:128], T.ec[:, 0:192], False, False)
+    mm(ps[3][:, 0:64], T.el[:, 0:128], T.er[:, 0:64], True, False)
+    mm(ps[3][:, 0:64], T.er[:, 0:128], T.ec[:, 192:256], False, False)
+    mm(ps[0][:, 0:256], T.zb[0:16, 0:128], T.er[:, 0:256], True, False)
+    mm(ps[0][:, 0:193], T.el[:, 256:384], T.er[:, 0:193], False, False)
     tab1, tab2, kd, t_ost = new(), new(), new(), new()
 
     def rows(tb, parts, a, b, ld, sm, src, tok):
         landed("y", sm, src)
         dsig(Y.dma_start(tb[parts, a:b], ld), tok)
-    w("y", c_pt, nm1)
-    for j, x in enumerate((T.nmb[:, 0:256], T.nmb[:, 256:512], T.pt[:, :])):
+    w("y", kw0)
+    dsig(Y.dma_start(T.wn[:, 512:1024], T.wn[:, 0:512]), kd)
+    w("y", c_pt, nm0, nm1)
+    for j, x in enumerate((T.onh[:, :], T.nmb[:, :], T.pt[:, :])):
         dsig(Y.dma_start(T.ost[j], x), t_ost)
+    w("y", kc0)
+    for a in (256, 512, 768):
+        dsig(Y.dma_start(T.c32[:, a:a + 256], T.c32[:, 0:256]), kd)
 
     w("s", t_sc, c_nxt)
     w("v", t_sc, c_nxt)
@@ -307,160 +326,180 @@ def rank_program(g, core, T, topo):
             sig(S.activation(o, src, F.Copy) if hh else V.tensor_copy(o, src), t)
         gt.append(t)
     t_st = []
-    for hh in range(2):
-        w("y", gt[2 * hh], gt[2 * hh + 1])
-        t_st.append(dsig(Y.dma_start(T.st[hh], T.gat[0:128:8, 64 + 2048 * hh:2112 + 2048 * hh])))
-        w("g", t_st[hh])
-        send(d1, T.la1[hh], T.st[hh], "la1%d" % hh)
-        send(d2, T.la2[hh], T.st[hh], "la2%d" % hh)
-    ks = sig(iota(T.sl[:, :], [[16, 64]]))
-    sig(put(view(ZN, 15), 8, 1.0 / 256), k4)
-    sig(put(view(FN, RN), 5, 1.0), k4)
+    for k, (a, b) in enumerate(PIECES):
+        w("y", *gt[a:b])
+        t_st.append(dsig(Y.dma_start(T["st%d" % k][:, :], T.gat[0:128:8, 64 + 1024 * a:64 + 1024 * b])))
+        w("g", t_st[k])
+        send(d1, T["la1%d" % k][:, :], T["st%d" % k][:, :], "la1%d_s" % k)
+    for k in range(len(PIECES)):
+        send(d2, T["la2%d" % k][:, :], T["st%d" % k][:, :], "la2%d_s" % k)
+    k7, k8 = new(), new()
+    sig(put(view(ZN, 15), 0, 4096.0), k7)
+    sig(put(view(FN, RN), 4, 128.0), k7)
+    sig(put(view(Z1, 15), 0, 1.0), k4)
+    w("g", k7)
+    sig(put(view(ZN, 15), 8, 64.0), k4)
+    sig(put(view(FN, RN), 5, 1.0), k8)
     sig(put(view(FP, RS), 2, 1.0), k4)
-    sig(put(view(FR, RS), RS, 1.0), k4)
     sig(put(view(FN, RS), 6, 1.0), k4)
-    w("g", kso)
-    sig(g.affine_select(cy(FT), cy(SO), [[1, 128]], A.is_ge, 0.0, 0, -1), k6)
-    sig(g.affine_select(cy(FS), cy(SO), [[-1, 128]], A.is_gt, 0.0, 0, 1), k6)
-    sig(iota(T.rw[:, :], [[16, 64]], 264, 1), k6)
+    w("g", k8)
+    sig(put(view(FN, RN), RF, -16384.0), k4)
     w("y", t_ost)
     for j in range(3):
         dsig(Y.dma_start(T.dat[4 + j:128:16, 64:TW], T.ost[j]), tab1)
-    rows(T.dat, slice(2, 128, 16), 64, TW, T.lpt1[:, :], "lpt1_s", s1, tab1)
-    rows(T.dat, slice(RS, 128, 16), 64, TW, T.lpt3[:, :], "lpt3_s", s3, tab1)
-    for hh in range(2):
-        rows(T.dat, slice(0, 128, 8), 64 + 2048 * hh, 2112 + 2048 * hh, T.la1[hh], "la1%d" % hh, s1, tab1)
+    Y.wait_ge(T.sem.lpt_s, 3 * len(eng))
+    dsig(Y.dma_start(T.dat[2:128:16, 64:TW], T.lpt1[:, :]), tab1)
+    dsig(Y.dma_start(T.dat[RS:128:16, 64:TW], T.lpt3[:, :]), tab1)
+    for k, (a, b) in enumerate(PIECES):
+        rows(T.dat, slice(0, 128, 8), 64 + 1024 * a, 64 + 1024 * b, T["la1%d" % k][:, :], "la1%d_s" % k, s1, tab1)
 
-    m_cd, t_nb, twq = [new(), new()], new(), new()
-    w("p", kz)
-    for j in range(4):
+    twq = new()
+
+    def quarter(out, j):
         w("p", gt[j])
         for kk in range(16):
-            m = mm(ps[6 + j // 2][:, 64 * (j % 2):64 * (j % 2) + 64], T.zm[:, 128 * kk:128 * kk + 128],
-                   T.gat[:, 64 + 1024 * j + kk:64 + 1024 * j + 1024:16], kk == 0, kk == 15)
-        if j % 2:
-            sig(m, m_cd[j // 2])
-    w("y", m_cd[0], m_cd[1], *t_st)
-    rows(T.gat, slice(RS, 128, 16), 64, TW, T.lpt2[:, :], "lpt2_s", s2, tab2)
-    for hh in range(2):
-        rows(T.gat, slice(0, 128, 8), 64 + 2048 * hh, 2112 + 2048 * hh, T.la2[hh], "la2%d" % hh, s2, tab2)
-    cv = new()
-    for hh in range(2):
-        w("v", m_cd[hh])
-        sig(V.tensor_scalar(T.nb[:, 8 + 128 * hh:136 + 128 * hh], ps[6 + hh][:, 0:128], -1.0 / 32, 128.26, A.mult, A.add), t_nb)
-        w("s", t_nb)
-        sig(S.activation(T.wq[:, 128 * hh:128 * hh + 128], ps[6 + hh][:, 0:128], F.Identity, bias=-8.25), twq)
-        if not hh:
-            sig(S.activation(T.wn[:, 0:1024], T.zb[:, 0:1024], F.Identity, bias=30000.0), kd)
-            sig(V.tensor_scalar(T.colN[:, :], T.p16[:, :], -1.0, None, A.mult), cv)
-            sig(V.tensor_scalar(T.colF[:, :], T.p16[:, :], RN, -1.0, A.is_equal, A.mult), cv)
+            m = mm(out, T.zm[:, 128 * kk:128 * kk + 128], T.gat[:, 64 + 1024 * j + kk:64 + 1024 * j + 1024:16], kk == 0, kk == 15)
+        return m
+    w("p", kz)
+    for j in range(3):
+        m = quarter(ps[6][:, 64 * j:64 * j + 64], j)
+    m_cd = [sig(m)]
+    w("v", m_cd[0])
+    t_nb = sig(V.tensor_scalar(T.nb[:, 8:200], ps[6][:, 0:192], -1.0 / 32, 128.26, A.mult, A.add))
 
+    w("p", gt[3])
+    for kk in range(16):
+        mm(ps[0][:, 193:256], cy(SF), T.gat[:, 3136 + kk:TW - 16:16], False, False)
     w("p", t_nb, zz)
-    m_c = sig(mm(ps[0][:, 0:257], cy(SL), T.nb[:, 7:264], False, True))
-    m_x = sig(mm(ps[2][:, 0:256], cy(ON4), T.nb[:, 8:264], False, True))
+    m_c = sig(mm(ps[0][:, 0:193], cy(SL), T.nb[:, 7:200], False, True))
+    m_x = [sig(mm(ps[2][:, 0:192], cy(ON4), T.nb[:, 8:200], False, True))]
+    for kk in range(16):
+        m = mm(ps[3][:, 0:64], cy(SG), T.gat[:, 3136 + kk:TW:16], False, kk == 15)
+    m_x.append(sig(m))
+    m_cd.append(sig(quarter(ps[7][:, 0:64], 3)))
+    w("y", m_cd[1], *t_st)
+    dsig(Y.dma_start(T.gat[RS:128:16, 64:TW], T.lpt2[:, :]), tab2)
+    for k, (a, b) in enumerate(PIECES):
+        rows(T.gat, slice(0, 128, 8), 64 + 1024 * a, 64 + 1024 * b, T["la2%d" % k][:, :], "la2%d_s" % k, s2, tab2)
+    sig(S.activation(T.mk[:, MK:1024], T.zb[:, MK:1024], F.Silu), t_mk)
+    w("s", t_nb)
+    sig(S.activation(T.wq[:, 0:192], ps[6][:, 0:192], F.Identity, bias=-8.25), twq)
+    w("s", m_cd[1])
+    sig(S.activation(T.wq[:, 192:256], ps[7][:, 0:64], F.Identity, bias=-8.25), twq)
     w("v", kx)
-    zxh = sig(V.tensor_copy(T.zx[:, :], cz(ZX, 288)))
-    t_mk = sig(S.activation(T.mk[:, 0:1024], T.zb[:, 0:1024], F.Silu))
+    zxh = sig(V.tensor_copy(T.zx[:, :], cz(ZX, 144)))
+    cv = sig(V.tensor_scalar(T.colF[:, :], T.p16[:, :], RN, -1.0, A.is_equal, A.mult))
+    sig(V.tensor_scalar(T.colI[:, :], T.p16[:, :], 2.0, 240.0, A.mult, A.add), cv)
+    sig(V.tensor_copy(T.yb[:, 0:8], T.zb[:, 0:8]), cv)
     w("v", m_c)
-    ta = sig(V.tensor_tensor_scan(T.ax[:, :], ps[0][:, 0:257], T.zb[:, 0:257], 0.0, A.add, A.add))
-    w("v", ta, m_x)
-    t = sig(V.tensor_tensor(T.oy[:, :], T.ax[:, 0:256], ps[2][:, 0:256], A.max))
-    w("v", t, kd0)
-    t = sig(V.tensor_tensor_scan(T.oh[:, :], T.d0[:, :], T.oy[:, :], 0.0, A.add, A.min))
+    ta = sig(V.tensor_tensor_scan(T.ax[:, 0:256], ps[0][:, 0:256], T.zb[:, 0:256], 0.0, A.add, A.add))
+    toy, t = [], new()
+    for j, (a, b) in enumerate(((0, 192), (192, 256))):
+        w("v", ta, m_x[j])
+        toy.append(sig(V.tensor_tensor(T.oy[:, a:b], T.ax[:, a:b], ps[2 + j][:, 0:b - a], A.max)))
+    for j, (a, b) in enumerate(((0, 192), (192, 256))):
+        w("v", toy[j], kd0)
+        sig(V.tensor_tensor_scan(T.oh[:, a:b], T.d0[:, a:b], T.oy[:, a:b], 0.0, A.add, A.min), t)
     w("v", t)
     tol = sig(V.tensor_copy(T.ol[:, :], T.oh[:, 15:256:16]))
-    w("v", tol, twq, kd)
+    w("v", tol, twq, kd, kw0, kc0)
     t = sig(V.tensor_copy(T.wn[:, :].indirect(T.ol[:, :]), T.wq[:, :]))
-    w("v", t, kc32)
+    w("v", t)
     t = sig(V.tensor_tensor_scan(T.dd[:, :], T.wn[:, 0:1024], T.c32[:, :], 100.0, A.min, A.add))
     w("v", t)
     tdc = sig(V.tensor_scalar(T.dc[:, :], T.dd[:, :], -8.0, 8.0, A.max, A.min))
-    w("p", tdc, zxh, nm1)
-    m_l2 = fold(ps[5][:, 0:64], T.zx, 0, T.dc)
+    w("p", zxh, nm1)
+    for j in range(3):
+        mm(ps[5][:, 0:64], T.el[:, 128:256], T.er[:, 0:64], j == 0, False)
+    w("p", tdc)
+    m_l2 = fold(ps[5][:, 0:64], T.zx, 0, T.dc, first=False)
     w("s", tol, t_mk, kcf)
     tmk = sig(S.activation(T.mk[:, :].indirect(T.ol[:, :]), T.cf[:, :], F.Silu))
-    w("v", tmk)
-    tcm = sig(V.tensor_tensor_scan(T.cm[:, :], T.mk[:, 0:1024], T.mk[:, 0:1024], CB, A.max, A.max))
-    fw, ttm, kq = new(), new(), new()
-    w("s", ta, cv)
-    sig(S.activation(T.totm[:, :], T.ax[:, 256:257], F.Identity, bias=T.colN[:, :]), ttm)
-    sig(S.activation(cy(IC), cy(I4), F.Copy, scale=1024.0), kq)
+    fw, kq = new(), new()
+    w("s", tmk)
+    tmb = sig(S.activation(T.mb[:, :], T.mk[:, 0:1024], F.Identity, bias=-CB))
+    w("v", tmb)
+    tcm = sig(V.tensor_tensor_scan(T.cm[:, :], T.mb[:, :], T.mb[:, :], 0.0, A.max, A.max))
+    zy = new()
+    for x, a, b in ((T.dat, 0, 64), (T.gat, 0, 64), (T.fl4, 0, 8)):
+        sig(S.activation(x[:, a:b], T.zb[:, 0:b - a], F.Copy), zy)
+    w("s", cv)
+    sig(S.activation(cy(IC), cy(I4), F.Copy, scale=0.25), kq)
+    sig(S.activation(cy(IM), cy(I4), F.Copy, scale=-2097152.0), kq)
+    w("s", k6, kt)
+    sig(S.activation(T.cy[:, FT:FT + 256], T.cy[:, WT:WT + 256], F.Copy, scale=-1.0 / 32), fw)
+    tyt = sig(S.activation(T.yt[:, :], T.y0[:, :], F.Identity, bias=T.colI[:, :]))
     sig(S.activation(T.win[:, 0:264], T.zb[:, 0:264], F.Identity, bias=T.colF[:, :]), fw)
     w("v", m_l2)
-    txi = sig(V.tensor_scalar(T.xi[:, :], ps[5][:, 0:64], 32768.0, None, A.add))
-    w("v", ttm, ks)
-    ttk = sig(V.tensor_scalar(T.tk[:, :], T.sl[:, :], T.totm[:, :], None, A.is_ge))
-    w("v", txi)
-    txp = sig(V.tensor_scalar(T.xp[:, :], T.xi[:, :], 4095, None, A.bitwise_and))
-    w("s", txi)
-    tpb = sig(S.activation(T.pb[:, :], ps[5][:, 0:64], F.Identity, bias=136.5001, scale=1.0 / 4096))
-    w("v", txp)
-    tll = sig(V.tensor_copy(T.ll[:, 0:64], T.xp[:, :]))
+    tpb = sig(V.tensor_scalar(T.pb[:, :], ps[5][:, 0:64], -2047.5, None, A.add))
+    tih = sig(V.tensor_scalar(T.ih[:, 0:128], cy(I4), 4.0, None, A.mult))
+    w("v", tpb)
+    tll = sig(V.tensor_tensor_scan(T.ll[:, 0:64], ps[5][:, 0:64], T.pb[:, :], 0.0, A.max, A.subtract))
+    ttk = sig(V.tensor_scalar(T.tk[:, :], T.pb[:, :], XB + 65000.0, None, A.is_ge))
 
     def pick(q, win, lst, at_, u, v, out, tok, *toks):
         w(q, *toks)
         src, o = win.indirect(lst[:, at_ + u:at_ + v]), out[:, 16 * u:16 * v]
         sig(V.tensor_copy(o, src) if q == "v" else S.activation(o, src, F.Copy), tok)
     tng, tr1, tr2 = [new(), new()], new(), new()
-    pick("v", T.dat[:, 64:TW], T.ll, 0, 0, R1, T.r1, tr1, tll, tab1)
-    pick("s", T.dat[:, 64:TW], T.ll, 0, R1, 64, T.r1, tr1, tll, tab1)
-    w("p", tcm, kq)
-    fold(ps[3][:, 0:64], T.zx, 144, T.cm, False)
+    w("p", tcm, kq, k4)
+    fold(ps[3][:, 0:64], T.cz, Z1, T.cm, False)
     w("p", tpb)
     m_lo = sig(mm(ps[3][:, 0:64], cy(IC), T.pb[:, :], False, True))
-    w("p", tr1, ta, k4)
-    m_l3 = fold(ps[0][:, 0:64], T.cz, ZN, T.r1)
+    pick("v", T.dat[:, 64:TW], T.ll, 0, 0, R1, T.r1, tr1, tll, tab1, zy)
+    pick("s", T.dat[:, 64:TW], T.ll, 0, R1, 64, T.r1, tr1, tll, tab1, zy)
+    w("p", ttk, ta)
+    mm(ps[0][:, 0:64], cy(IM), T.tk[:, :], True, False)
+    w("p", tr1)
+    m_l3 = fold(ps[0][:, 0:64], T.cz, ZN, T.r1, first=False)
     w("v", m_lo)
-    tll0 = sig(V.tensor_scalar(T.ll[:, 64:128], ps[3][:, 0:64], -129.0 * 256 - CB, 4095.0, A.add, A.min))
-    w("s", ttk)
-    tth = sig(S.activation(T.thr[:, :], T.tk[:, :], F.Copy, scale=64.0))
+    tll0 = sig(V.tensor_scalar(T.ll[:, 64:128], ps[3][:, 0:64], -XB / 16, 4095.0, A.add, A.min))
+    sig(V.tensor_scalar(T.ih[:, 128:256], cy(I4), -4.0, None, A.mult), tih)
     pick("v", T.dat[:, 64:TW], T.ll, 64, 0, N1, T.ng, tng[0], tll0)
     pick("s", T.dat[:, 64:TW], T.ll, 64, N1, 64, T.ng, tng[1], tll0)
     w("v", m_l3)
-    tl3 = sig(V.tensor_scalar(T.l3[:, :], ps[0][:, 0:64], 256.0, None, A.mult))
-    pick("v", T.gat[:, :], T.l3, 0, 0, R2, T.r2, tr2, tl3, tab2, zz)
-    pick("s", T.gat[:, :], T.l3, 0, R2, 64, T.r2, tr2, tl3, tab2, zz)
+    tl3 = sig(V.tensor_scalar(T.l3[:, :], ps[0][:, 0:64], 1.0 / 64, None, A.mult))
+    pick("v", T.gat[:, :], T.l3, 0, 0, R2, T.r2, tr2, tl3, tab2)
+    pick("s", T.gat[:, :], T.l3, 0, R2, 64, T.r2, tr2, tl3, tab2)
     w("p", twq)
     mm(ps[6][:, :], cz(FP), T.r1[:, 0:512], True, False)
     mm(ps[7][:, :], cz(FP), T.r1[:, 512:1024], True, False)
     w("p", tng[0], tng[1])
     m_ac = sig(mm(ps[6][:, :], cz(FN), T.ng[:, 0:512], False, True))
-    mm(ps[7][:, :], cz(FN), T.ng[:, 512:1024], False, False)
+    m_ad = sig(mm(ps[7][:, :], cz(FN), T.ng[:, 512:1024], False, True))
     w("p", tr2)
     m_l4 = fold(ps[1][:, 0:64], T.cz, ZN, T.r2)
-    m_ad = sig(mm(ps[7][:, :], cz(FR), T.r2[:, 512:1024], False, True))
-    w("v", m_ac, tr2)
-    tfd = [sig(V.tensor_tensor(T.fd[:, 0:512], ps[6][:, :], T.r2[:, 0:512], A.add))]
+    tfd = [new(), new()]
+
+    def sums(a, b):
+        w("v", m_ac, m_ad, tr2)
+        sig(V.tensor_tensor(T.fd[:, a:b], ps[6 + a // 512][:, a % 512:(b - 1) % 512 + 1], T.r2[:, a:b], A.add), tfd[a // 512])
+    sums(0, 512)
+    if FA > 512:
+        sums(512, FA)
 
     w("v", m_l4)
-    tl5 = sig(V.tensor_scalar(T.l5[:, :], ps[1][:, 0:64], 256.0, None, A.mult))
-    w("v", tth)
-    f4 = sig(V.tensor_tensor(T.fl4[:, 8:72], ps[1][:, 0:64], T.thr[:, :], A.is_gt))
-    x2 = sig(V.tensor_tensor(T.xn[:, :], ps[1][:, 0:64], T.thr[:, :], A.is_le))
-    w("s", tl5, zz)
-    tr3 = [sig(S.activation(T.r3[:, 0:512], T.dat[:, :].indirect(T.l5[:, 0:32]), F.Copy))]
-    w("p", f4, zz, tol, k6)
+    w("v", tyt)
+    tl5 = sig(V.tensor_scalar(T.l5[:, :], ps[1][:, 0:64], 1.0 / 64, None, A.mult))
+    f4 = sig(V.tensor_scalar(T.fl4[:, 8:72], ps[1][:, 0:64], 0.0, None, A.is_gt))
+    sig(V.tensor_tensor(T.yb[:, 8:72], ps[1][:, 0:64], T.yt[:, :], A.min), f4)
+    w("s", tl5)
+    parts = ((0, PA), (PA, 64))
+    tr3 = [sig(S.activation(T.r3[:, 16 * u:16 * v], T.dat[:, :].indirect(T.l5[:, u:v]), F.Copy)) for u, v in parts]
+    sums(FA, FB)
+    w("p", f4, zy, tol, fw, tih)
     mm(ps[2][:, 0:64], cy(FS), T.fl4[:, 7:71], True, False)
-    m_a = sig(mm(ps[2][:, 0:64], cy(FT), T.fl4[:, 8:72], False, True))
-    w("s", m_ad)
-    tfd.append(sig(S.activation(T.fd[:, 512:1024], ps[7][:, :], F.Copy)))
-    tr3.append(sig(S.activation(T.r3[:, 512:1024], T.dat[:, :].indirect(T.l5[:, 32:64]), F.Copy)))
-    w("v", x2, k6)
-    x3 = sig(V.tensor_tensor(T.xx[:, :], T.xn[:, :], T.rw[:, :], A.mult))
+    mm(ps[2][:, 0:64], cy(FT), T.fl4[:, 8:72], False, False)
+    mm(ps[2][:, 0:64], T.ih[:, 0:128], T.yb[:, 7:71], False, False)
+    m_a = sig(mm(ps[2][:, 0:64], T.ih[:, 128:256], T.yb[:, 8:72], False, True))
     w("v", m_a)
-    q1 = sig(V.tensor_tensor_scan(T.a4[:, :], ps[2][:, 0:64], T.zb[:, 0:64], 0.0, A.add, A.add))
-    w("v", q1, x3)
-    q3 = sig(V.tensor_tensor(T.o4[:, :], T.a4[:, :], T.xx[:, :], A.max))
-    w("v", q3)
-    q5 = sig(V.tensor_copy(T.l4[:, :], T.o4[:, :]))
+    q5 = sig(V.tensor_tensor_scan(T.l4[:, :], ps[2][:, 0:64], T.c32[:, 0:64], T.colI[:, :], A.add, A.add))
+    sums(FB, 1024)
     w("v", q5, fw)
-    tw = None
-    for hh in range(2):
-        w("v", tfd[hh], tr3[hh])
-        if tw:
-            w("v", tw)
-        tw = sig(V.tensor_tensor(T.win[:, :].indirect(T.l4[:, 32 * hh:32 * hh + 32]), T.fd[:, 512 * hh:512 * hh + 512],
-                                 T.r3[:, 512 * hh:512 * hh + 512], A.add))
+    tw = new()
+    for (u, v), t in zip(parts, tr3):
+        w("v", tfd[0], tfd[(v - 1) // 32], t, tw)
+        sig(V.tensor_tensor(T.win[:, :].indirect(T.l4[:, u:v]), T.fd[:, 16 * u:16 * v], T.r3[:, 16 * u:16 * v], A.add), tw)
     w("y", tw)
     t_y = new()
     w("s", tw)

from concourse.bass import DstId, RemoteDMATransfer
from concourse.mybir import AluOpType as A, ActivationFunctionType as F

BF, F32, F16, I32, U16 = "bfloat16", "float32", "float16", "int32", "uint16"
TW = 4160
SCRATCH = {
    "own_i": ("sbuf", [128, 256], I32), "nxt_i": ("sbuf", [128, 256], I32), "pts_i": ("sbuf", [128, 256], I32),
    "own_u": ("sbuf", [128, 256], U16), "nxt_u": ("sbuf", [128, 256], U16), "own_r": ("sbuf", [128, 256], U16),
    "nf": ("sbuf", [128, 256], F32), "onh": ("sbuf", [128, 256], BF), "nmb": ("sbuf", [128, 256], BF),
    "ptsb": ("sbuf", [128, 256], BF), "zb": ("sbuf", [128, 1040], BF),
    "tab": ("sbuf", [128, 16384], BF), "dat": ("sbuf", [128, TW], BF), "gat": ("sbuf", [128, TW], BF),
    "pidx": ("sbuf", [128, 1], I32), "p16": ("sbuf", [128, 1], I32),
    "colA": ("sbuf", [128, 1], F32), "colB": ("sbuf", [128, 1], F32), "colC": ("sbuf", [128, 1], F32),
    "colF": ("sbuf", [128, 1], F32), "colI": ("sbuf", [128, 1], F32),
    "io64": ("sbuf", [128, 64], BF), "lb": ("sbuf", [128, 64], F32),
    "cz": ("sbuf", [128, 688], BF), "cy": ("sbuf", [128, 1792], BF), "i32": ("sbuf", [128, 128], F32),
    "zm": ("sbuf", [128, 2048], BF), "ep": ("sbuf", [8, 144], BF), "zx": ("sbuf", [128, 144], F16),
    "er": ("sbuf", [16, 256], BF), "ec": ("sbuf", [16, 256], BF), "el": ("sbuf", [16, 384], BF),
    "d0": ("sbuf", [128, 256], BF), "c32": ("sbuf", [128, 1024], BF),
    "cio": ("sbuf", [16, 256], BF), "cf": ("sbuf", [128, 256], F32), "yt": ("sbuf", [128, 64], F32),
    "mk": ("sbuf", [128, 1280], F32), "wn": ("sbuf", [128, 1280], F32),
    "pr8": ("sbuf", [8, 4096], BF), "pt": ("sbuf", [128, 256], BF),
    "ng": ("sbuf", [128, 1024], BF), "nb": ("sbuf", [128, 272], BF),
    "ax": ("sbuf", [128, 257], F32), "oy": ("sbuf", [128, 256], F16), "oh": ("sbuf", [128, 256], F16),
    "wq": ("sbuf", [128, 256], F32), "ol": ("sbuf", [128, 16], U16), "cm": ("sbuf", [128, 1024], BF),
    "mb": ("sbuf", [128, 1024], BF),
    "dd": ("sbuf", [128, 1024], F16), "dc": ("sbuf", [128, 1024], F16),
    "tk": ("sbuf", [128, 64], BF), "pb": ("sbuf", [128, 64], BF),
    "ll": ("sbuf", [128, 128], U16), "l3": ("sbuf", [128, 64], U16), "l4": ("sbuf", [128, 64], U16),
    "l5": ("sbuf", [128, 64], U16),
    "r1": ("sbuf", [128, 1024], BF), "r2": ("sbuf", [128, 1024], BF), "r3": ("sbuf", [128, 1024], F32),
    "fl4": ("sbuf", [128, 72], BF), "yb": ("sbuf", [128, 72], F16),
    "ih": ("sbuf", [128, 256], F16), "y0": ("sbuf", [128, 64], F32), "a4": ("sbuf", [128, 64], F32),
    "fd": ("sbuf", [128, 1024], F32), "win": ("sbuf", [128, 2688], F32),
    "lpt1": ("dram", [128, 256], BF), "lpt2": ("dram", [128, 256], BF), "lpt3": ("dram", [128, 256], BF),
    "pst": ("dram", [128, 256], BF), "ost": ("dram", [3, 128, 256], BF),
}
for _b in range(8):
    SCRATCH["ps%d" % _b] = ("psum", [128, 512], F32)
PIECES = ((0, 2), (2, 3), (3, 4))
for _k, (_a, _b) in enumerate(PIECES):
    for _nm in ("st", "la1", "la2"):
        SCRATCH["%s%d" % (_nm, _k)] = ("dram", [128, 128 * (_b - _a)], BF)
NE = 130
SEMAPHORES = (["own0_s", "own_r_s", "lpt_s", "ls"] + ["e%d" % _i for _i in range(NE)]
              + ["la%d%d_s" % (_d, _k) for _d in (1, 2) for _k in range(len(PIECES))])

ZN, ZX, Z1, FN, FP = 0, 144, 288, 432, 560
XB = 3 * 262144.0 - 32768
CB = 32.0
I4, IL, FO, WT, WS, FT, FS, SL, SF, ON4, SG, IB, IC, IM = (128 * _k for _k in range(14))
TG0, TG, TD, TS = 704, 1344, 5376, 5056
VA = (768, 512, 512, 256)
AE = 1536
MK, PA = 896, 20
FA, FB = 512, 832
N1, R1, R2 = 28, 32, 32
RN, RS, RF = 10, 9, 12


def rank_program(g, core, T, topo):
    r = T.rank_of(core)
    if r is None:
        return
    n = len(T.cores)
    d1, d2, d3 = (T.cores[(r - k) % n] for k in (1, 2, 3))
    s1, s2, s3 = (T.cores[(r + k) % n] for k in (1, 2, 3))
    V, S, P, Y = g.vector, g.scalar, g.tensor, g.sync
    Q = {"g": g, "v": V, "s": S, "p": P, "y": Y}
    ctr, seen, waited, made, ls = [0], {}, {}, [], [0]

    def new():
        t = ["e%d" % ctr[0], 0]
        ctr[0] += 1
        made.append(t)
        return t

    def sig(ins, t=None, by=1):
        t = t or new()
        ins.then_inc(T.sem[t[0]], by)
        t[1] += by
        return t

    def dsig(ins, t=None):
        return sig(ins, t, 16)

    def w(q, *toks):
        for t in toks:
            if seen.get((q, t[0]), 0) < t[1]:
                Q[q].wait_ge(T.sem[t[0]], t[1])
                seen[(q, t[0])] = t[1]
                waited[t[0]] = t[1]

    def landed(q, nm, src):
        Q[q].wait_ge(T.sem[nm], len(topo.engines(src, core)))

    def send(dst, out, in_, sem):
        rid, pid = topo.addr(dst)[:2]
        eng = topo.engines(core, dst)
        g.remote_dma(out_ap=out, in_ap=in_, remote_sem=T.sem[sem], local_sem=T.sem.ls, pid=pid, routing_id=rid,
                     dma_engine_mask=sum(1 << e for e in eng))
        ls[0] += len(eng)

    def iota(out, pattern, base=0, cm=0):
        return g.iota(out, pattern, base, cm, allow_small_or_imprecise_dtypes=True)

    def cz(b, width=128):
        return T.cz[:, b:b + width]

    def cy(b):
        return T.cy[:, b:b + 128]

    def mm(out, lhsT, rhs, first, last):
        return P.matmul(out, lhsT, rhs, first, last)

    def fold(out, mat, at_, rows_, last=True, first=True):
        for k in range(16):
            m = mm(out, mat[:, at_ + 15 - k:at_ + 143 - k], rows_[:, k:1024:16], first and k == 0, last and k == 15)
        return sig(m) if last else None

    ps = [T["ps%d" % b] for b in range(8)]

    t_own = dsig(Y.dma_start(T.own_i[:, :], T.own[:, :]))
    t_pts = dsig(Y.dma_start(T.pts_i[:, :], T.pts[:, :]))
    t_nxt = dsig(Y.dma_start(T.nxt_i[:, :], T.nxt[:, :]))

    k0, f_tab, f_tabv, t_tab = new(), new(), new(), new()
    sig(g.iota(T.pidx[:, :], [[0, 1]], 0, 1), k0)
    sig(iota(T.io64[:, :], [[1, 64]]), k0)
    sig(iota(T.tab[:, 0:TG0], [[0, TG0]]), f_tab)

    z00 = sig(V.memset(T.zb[:, 0:256], 0.0))
    z0 = sig(V.memset(T.zb[:, 256:1040], 0.0))
    w("s", z00)
    a = TG + TD
    for _ in range(2):
        sig(S.activation(T.tab[:, a:a + 256], T.zb[:, 0:256], F.Copy), f_tab)
        a += 256
    w("s", z0)
    for a in range(a, TG + TD + TS, 1024):
        b = min(a + 1024, TG + TD + TS)
        sig(S.activation(T.tab[:, a:b], T.zb[:, 0:b - a], F.Copy), f_tab)
    w("y", z00, z0)
    for a in range(TG, TG + TD, 1024):
        b = min(a + 1024, TG + TD)
        dsig(Y.dma_start(T.tab[:, a:b], T.zb[:, 0:b - a]), t_tab)
    at = [TG + TD + TS]

    def zeros(width):
        sig(V.memset(T.tab[:, at[0]:at[0] + width], 0.0), f_tabv)
        at[0] += width

    w("v", k0)
    c1 = sig(V.tensor_scalar(T.p16[:, :], T.pidx[:, :], 15, None, A.bitwise_and))
    zeros(VA[0])
    w("v", c1)
    cc = new()
    sig(V.tensor_scalar(T.colB[:, :], T.p16[:, :], 8, None, A.is_equal), cc)
    sig(V.tensor_scalar(T.colA[:, :], T.p16[:, :], 0, None, A.is_equal), cc)
    zeros(VA[1])
    w("v", cc)
    c2 = sig(V.tensor_scalar(T.colC[:, :], T.p16[:, :], RF, T.colA[:, :], A.is_equal, A.add))
    zeros(VA[3])
    w("v", t_own)
    c_own = [sig(V.tensor_copy(T.own_u[:, a:b], T.own_i[:, a:b])) for a, b in ((0, AE // 16), (AE // 16, 256))]
    w("v", c2)
    b1 = sig(V.tensor_scalar(T.lb[:, :], T.io64[:, :], T.colA[:, :], None, A.mult))
    da = sig(V.tensor_scalar(T.dat[:, 64:128], T.io64[:, :], T.colB[:, :], T.colC[:, :], A.mult, A.add))
    c_nf = sig(V.tensor_copy(T.nf[:, :], T.own_i[:, :]))
    w("v", b1)

    def double(to, frm, width):
        w("v", da)
        k = (to - frm) // 64
        sig(V.tensor_scalar(T.dat[:, 64 + to:64 + to + width], T.dat[:, 64 + frm:64 + frm + width], T.lb[:, k:k + 1], None,
                            A.add), da)
    double(64, 0, 64)
    zeros(VA[2])
    double(128, 0, 128)
    w("v", t_pts)
    c_pts = sig(V.tensor_copy(T.ptsb[:, :], T.pts_i[:, :]))
    double(256, 0, 256)
    zeros(512)
    double(512, 0, 512)
    zeros(512)
    double(1024, 0, AE - 1024)
    zeros(16384 - at[0])
    w("v", t_nxt)
    c_nxt = sig(V.tensor_copy(T.nxt_u[:, :], T.nxt_i[:, :]))
    db = new()
    w("s", b1, da)
    for to, frm, width in ((AE, AE - 1024, 2048 - AE), (2048, 0, 1024), (3072, 0, 1024)):
        k = (to - frm) // 64
        sig(S.activation(T.dat[:, 64 + to:64 + to + width], T.dat[:, 64 + frm:64 + frm + width], F.Identity,
                         bias=T.lb[:, k:k + 1]), db)

    w("g", c_own[0])
    send(d1, T.own_r[:, 0:AE // 16], T.own_u[:, 0:AE // 16], "own0_s")
    w("g", c_own[1])
    send(d1, T.own_r[:, AE // 16:256], T.own_u[:, AE // 16:256], "own_r_s")
    sig(iota(T.tab[:, TG0:TG], [[0, TG - TG0]]), f_tab)

    w("v", f_tab, f_tabv, t_tab, da)
    landed("v", "own0_s", s1)
    t_s0 = sig(V.tensor_copy(T.tab[:, :].indirect(T.own_r[:, 0:AE // 16]), T.dat[:, 64:64 + AE]))
    landed("v", "own_r_s", s1)
    w("v", db, t_s0)
    t_sc = sig(V.tensor_copy(T.tab[:, :].indirect(T.own_r[:, AE // 16:256]), T.dat[:, 64 + AE:TW]))

    w("y", c_pts)
    landed("y", "own0_s", s1)
    t_pst = dsig(Y.dma_start(T.pst[:, :], T.ptsb[:, :]))
    landed("y", "own_r_s", s1)
    t_pr8 = dsig(Y.dma_start(T.pr8[:, :], T.ptsb[:, :]))
    t_zm = new()
    for a in (0, 1024):
        dsig(Y.dma_start(T.zm[:, a:a + 1024], T.zb[:, 0:1024]), t_zm)
    t_cz = dsig(Y.dma_start(T.cz[:, :], T.zb[:, 0:688]))

    def view(b, start):
        return T.cz[:, b + start:b + start + 113:16]

    def put(x, part, wt):
        return g.affine_select(x, x, [[-16, 8]], A.not_equal, wt, -part, 1)

    def setw(x, x0, pattern, wt, base, cm):
        return g.affine_select(x, x0, pattern, A.is_ge, wt, base, cm)
    grp = [[16, 8], [0, 16]]
    vx = view(ZX, 15)
    z128 = T.zb[:, 0:128]
    kz, kf, k3, k4, k6, ki = new(), new(), new(), new(), new(), new()
    w("g", z00, z0)
    sig(setw(cy(FO), z128, grp, -32.0, -1, -1), kf)
    sig(g.affine_select(cy(I4), z128, [[-1, 128]], A.not_equal, 0.25, 0, 1), ki)
    w("g", kf)
    sig(setw(cy(FO), cy(FO), grp, 0.0, 15, -1), kf)
    sig(g.affine_select(cy(IL), z128, [[-1, 128]], A.not_equal, 1.0 / 256, 0, 1), ki)
    w("g", kf)
    kt = sig(g.affine_select(cy(WT), cy(FO), [[1, 128]], A.is_ge, 0.0, 0, -1))
    k2 = sig(g.affine_select(T.ep[:, :], T.zb[0:8, 0:144], [[1, 144]], A.not_equal, 1.0, -15, -16))
    w("g", t_pst)
    eng = [e for e in topo.engines(core, d1) if e in topo.engines(core, d2) and e in topo.engines(core, d3)]
    g.remote_dma_fused([RemoteDMATransfer(dst_ids=[DstId(rid=topo.addr(d)[0], pnc=topo.addr(d)[1]) for d in (d1, d3, d2)],
                                          dma_engine_mask=sum(1 << e for e in eng), remote_sem=T.sem.lpt_s, src=T.pst[:, :],
                                          dsts=[T.lpt1[:, :], T.lpt3[:, :], T.lpt2[:, :]])], local_sem=T.sem.ls)
    ls[0] += len(eng)
    kl = sig(g.affine_select(cy(SL), z128, grp, A.not_equal, 1.0, 15, -1))
    sig(g.affine_select(cy(SF), z128, grp, A.not_equal, 1.0, RF, -1), kl)
    ke = sig(g.affine_select(T.er[:, :], T.zb[0:16, 0:256], [[0, 16], [1, 16]], A.not_equal, 1.0, 0, -1))
    k5 = sig(iota(T.cio[:, :], [[1, 256]]))
    w("g", k5)
    kc = sig(g.affine_select(T.ec[:, :], T.cio[:, :], [[0, 16], [1, 16]], A.is_equal, 0.0, 0, -1))
    kc0 = sig(iota(T.c32[:, 0:256], [[0, 256]], 32))
    w("g", t_cz)
    sig(setw(vx, vx, [[16, 8]], 256.0, -1, -1), k3)
    kcf = sig(iota(T.cf[:, :], [[1, 256]], int(CB)))
    w("g", k3)
    kx = sig(setw(vx, vx, [[16, 8]], 0.0, 15, -1))
    t_mk = sig(iota(T.mk[:, 0:MK], [[0, MK]]))
    sig(g.affine_select(cy(WS), cy(FO), [[-1, 128]], A.is_gt, 0.0, 0, 1), k6)
    sig(iota(T.y0[:, :], [[32, 64]], 32), k6)
    w("y", t_zm, ki, kt)
    for part, b in ((0, I4), (8, IL), (RF, WT)):
        dsig(Y.dma_start(T.zm[part:128:16, :], cy(b)), kz)

    zz, nm1, kr = new(), new(), new()
    w("p", t_pr8, k2)
    for kk in range(16):
        m = mm(ps[4][:, 0:256], T.ep[:, 15 - kk:143 - kk], T.pr8[:, kk:4096:16], kk == 0, kk == 15)
    m_pt = sig(m)
    w("s", c_nf)
    nm0 = sig(S.activation(T.onh[:, :], T.nf[:, :], F.Identity, bias=128.0, scale=1.0 / 128))
    w("s", ki)
    kb = new()
    sig(S.activation(T.i32[:, :], cy(I4), F.Copy, scale=-128.0), kb)
    sig(S.activation(cy(IB), cy(I4), F.Copy, scale=16384.0), kb)
    sig(S.activation(T.nb[:, 0:8], T.zb[:, 0:8], F.Identity, bias=128.0), zz)
    sig(S.activation(T.el[:, 128:256], T.zb[0:16, 0:128], F.Identity, bias=262144.0), kr)
    sig(S.activation(T.el[:, 256:384], T.zb[0:16, 0:128], F.Identity, bias=-128.0), kr)
    kw0 = sig(S.activation(T.wn[:, 0:512], T.zb[:, 0:512], F.Identity, bias=30000.0))
    w("s", m_pt)
    c_pt = sig(S.activation(T.pt[:, :], ps[4][:, 0:256], F.Copy))
    w("p", kb, nm0, c_nf)
    mm(ps[5][:, 0:256], T.i32[:, :], T.nf[:, :], True, False)
    m_nl = sig(mm(ps[5][:, 0:256], cy(IB), T.onh[:, :], False, True))
    w("s", kl)
    sig(S.activation(T.cy[:, ON4:ON4 + 256], T.cy[:, SL:SL + 256], F.Copy, scale=-2048.0), kr)
    w("s", m_nl)
    sig(S.activation(T.nmb[:, :], ps[5][:, 0:256], F.Identity, bias=16384.0, scale=-1.0 / 32), nm1)
    w("s", ke)
    sig(S.activation(T.el[:, 0:128], T.er[:, 0:128], F.Identity, bias=41984.0, scale=-40960.0), kr)
    w("p", c_pt, ke)
    m_d0 = sig(mm(ps[4][:, 0:256], T.er[:, 0:128], T.er[:, 0:256], True, True))
    w("s", m_d0)
    kd0 = sig(S.activation(T.d0[:, :], ps[4][:, 0:256], F.Copy, scale=2048.0))
    w("p", kr, kc)
    mm(ps[2][:, 0:192], T.el[:, 0:128], T.er[:, 0:192], True, False)
    mm(ps[2][:, 0:192], T.el[:, 128:256], T.er[:, 0:192], False, False)
    mm(ps[2][:, 0:192], T.er[:, 0:128], T.ec[:, 0:192], False, False)
    mm(ps[3][:, 0:64], T.el[:, 0:128], T.er[:, 0:64], True, False)
    mm(ps[3][:, 0:64], T.er[:, 0:128], T.ec[:, 192:256], False, False)
    mm(ps[0][:, 0:256], T.zb[0:16, 0:128], T.er[:, 0:256], True, False)
    mm(ps[0][:, 0:193], T.el[:, 256:384], T.er[:, 0:193], False, False)
    tab1, tab2, kd, t_ost = new(), new(), new(), new()

    def rows(tb, parts, a, b, ld, sm, src, tok):
        landed("y", sm, src)
        dsig(Y.dma_start(tb[parts, a:b], ld), tok)
    w("y", kw0)
    dsig(Y.dma_start(T.wn[:, 512:1024], T.wn[:, 0:512]), kd)
    w("y", c_pt, nm0, nm1)
    for j, x in enumerate((T.onh[:, :], T.nmb[:, :], T.pt[:, :])):
        dsig(Y.dma_start(T.ost[j], x), t_ost)
    w("y", kc0)
    for a in (256, 512, 768):
        dsig(Y.dma_start(T.c32[:, a:a + 256], T.c32[:, 0:256]), kd)

    w("s", t_sc, c_nxt)
    w("v", t_sc, c_nxt)
    gt = []
    for j in range(4):
        t = new()
        for hh in range(2):
            a = 1024 * j + 512 * hh
            o, src = T.gat[:, 64 + a:64 + a + 512], T.tab[:, :].indirect(T.nxt_u[:, a // 16:a // 16 + 32])
            sig(S.activation(o, src, F.Copy) if hh else V.tensor_copy(o, src), t)
        gt.append(t)
    t_st = []
    for k, (a, b) in enumerate(PIECES):
        w("y", *gt[a:b])
        t_st.append(dsig(Y.dma_start(T["st%d" % k][:, :], T.gat[0:128:8, 64 + 1024 * a:64 + 1024 * b])))
        w("g", t_st[k])
        send(d1, T["la1%d" % k][:, :], T["st%d" % k][:, :], "la1%d_s" % k)
    for k in range(len(PIECES)):
        send(d2, T["la2%d" % k][:, :], T["st%d" % k][:, :], "la2%d_s" % k)
    k7, k8 = new(), new()
    sig(put(view(ZN, 15), 0, 4096.0), k7)
    sig(put(view(FN, RN), 4, 128.0), k7)
    sig(put(view(Z1, 15), 0, 1.0), k4)
    w("g", k7)
    sig(put(view(ZN, 15), 8, 64.0), k4)
    sig(put(view(FN, RN), 5, 1.0), k8)
    sig(put(view(FP, RS), 2, 1.0), k4)
    sig(put(view(FN, RS), 6, 1.0), k4)
    w("g", k8)
    sig(put(view(FN, RN), RF, -16384.0), k4)
    w("y", t_ost)
    for j in range(3):
        dsig(Y.dma_start(T.dat[4 + j:128:16, 64:TW], T.ost[j]), tab1)
    Y.wait_ge(T.sem.lpt_s, 3 * len(eng))
    dsig(Y.dma_start(T.dat[2:128:16, 64:TW], T.lpt1[:, :]), tab1)
    dsig(Y.dma_start(T.dat[RS:128:16, 64:TW], T.lpt3[:, :]), tab1)
    for k, (a, b) in enumerate(PIECES):
        rows(T.dat, slice(0, 128, 8), 64 + 1024 * a, 64 + 1024 * b, T["la1%d" % k][:, :], "la1%d_s" % k, s1, tab1)

    twq = new()

    def quarter(out, j):
        w("p", gt[j])
        for kk in range(16):
            m = mm(out, T.zm[:, 128 * kk:128 * kk + 128], T.gat[:, 64 + 1024 * j + kk:64 + 1024 * j + 1024:16], kk == 0, kk == 15)
        return m
    w("p", kz)
    for j in range(3):
        m = quarter(ps[6][:, 64 * j:64 * j + 64], j)
    m_cd = [sig(m)]
    w("v", m_cd[0])
    t_nb = sig(V.tensor_scalar(T.nb[:, 8:200], ps[6][:, 0:192], -1.0 / 32, 128.26, A.mult, A.add))

    w("p", gt[3])
    for kk in range(16):
        mm(ps[0][:, 193:256], cy(SF), T.gat[:, 3136 + kk:TW - 16:16], False, False)
    w("p", t_nb, zz)
    m_c = sig(mm(ps[0][:, 0:193], cy(SL), T.nb[:, 7:200], False, True))
    m_x = [sig(mm(ps[2][:, 0:192], cy(ON4), T.nb[:, 8:200], False, True))]
    for kk in range(16):
        m = mm(ps[3][:, 0:64], cy(SG), T.gat[:, 3136 + kk:TW:16], False, kk == 15)
    m_x.append(sig(m))
    m_cd.append(sig(quarter(ps[7][:, 0:64], 3)))
    w("y", m_cd[1], *t_st)
    dsig(Y.dma_start(T.gat[RS:128:16, 64:TW], T.lpt2[:, :]), tab2)
    for k, (a, b) in enumerate(PIECES):
        rows(T.gat, slice(0, 128, 8), 64 + 1024 * a, 64 + 1024 * b, T["la2%d" % k][:, :], "la2%d_s" % k, s2, tab2)
    sig(S.activation(T.mk[:, MK:1024], T.zb[:, MK:1024], F.Silu), t_mk)
    w("s", t_nb)
    sig(S.activation(T.wq[:, 0:192], ps[6][:, 0:192], F.Identity, bias=-8.25), twq)
    w("s", m_cd[1])
    sig(S.activation(T.wq[:, 192:256], ps[7][:, 0:64], F.Identity, bias=-8.25), twq)
    w("v", kx)
    zxh = sig(V.tensor_copy(T.zx[:, :], cz(ZX, 144)))
    cv = sig(V.tensor_scalar(T.colF[:, :], T.p16[:, :], RN, -1.0, A.is_equal, A.mult))
    sig(V.tensor_scalar(T.colI[:, :], T.p16[:, :], 2.0, 240.0, A.mult, A.add), cv)
    sig(V.tensor_copy(T.yb[:, 0:8], T.zb[:, 0:8]), cv)
    w("v", m_c)
    ta = sig(V.tensor_tensor_scan(T.ax[:, 0:256], ps[0][:, 0:256], T.zb[:, 0:256], 0.0, A.add, A.add))
    toy, t = [], new()
    for j, (a, b) in enumerate(((0, 192), (192, 256))):
        w("v", ta, m_x[j])
        toy.append(sig(V.tensor_tensor(T.oy[:, a:b], T.ax[:, a:b], ps[2 + j][:, 0:b - a], A.max)))
    for j, (a, b) in enumerate(((0, 192), (192, 256))):
        w("v", toy[j], kd0)
        sig(V.tensor_tensor_scan(T.oh[:, a:b], T.d0[:, a:b], T.oy[:, a:b], 0.0, A.add, A.min), t)
    w("v", t)
    tol = sig(V.tensor_copy(T.ol[:, :], T.oh[:, 15:256:16]))
    w("v", tol, twq, kd, kw0, kc0)
    t = sig(V.tensor_copy(T.wn[:, :].indirect(T.ol[:, :]), T.wq[:, :]))
    w("v", t)
    t = sig(V.tensor_tensor_scan(T.dd[:, :], T.wn[:, 0:1024], T.c32[:, :], 100.0, A.min, A.add))
    w("v", t)
    tdc = sig(V.tensor_scalar(T.dc[:, :], T.dd[:, :], -8.0, 8.0, A.max, A.min))
    w("p", zxh, nm1)
    for j in range(3):
        mm(ps[5][:, 0:64], T.el[:, 128:256], T.er[:, 0:64], j == 0, False)
    w("p", tdc)
    m_l2 = fold(ps[5][:, 0:64], T.zx, 0, T.dc, first=False)
    w("s", tol, t_mk, kcf)
    tmk = sig(S.activation(T.mk[:, :].indirect(T.ol[:, :]), T.cf[:, :], F.Silu))
    fw, kq = new(), new()
    w("s", tmk)
    tmb = sig(S.activation(T.mb[:, :], T.mk[:, 0:1024], F.Identity, bias=-CB))
    w("v", tmb)
    tcm = sig(V.tensor_tensor_scan(T.cm[:, :], T.mb[:, :], T.mb[:, :], 0.0, A.max, A.max))
    zy = new()
    for x, a, b in ((T.dat, 0, 64), (T.gat, 0, 64), (T.fl4, 0, 8)):
        sig(S.activation(x[:, a:b], T.zb[:, 0:b - a], F.Copy), zy)
    w("s", cv)
    sig(S.activation(cy(IC), cy(I4), F.Copy, scale=0.25), kq)
    sig(S.activation(cy(IM), cy(I4), F.Copy, scale=-2097152.0), kq)
    w("s", k6, kt)
    sig(S.activation(T.cy[:, FT:FT + 256], T.cy[:, WT:WT + 256], F.Copy, scale=-1.0 / 32), fw)
    tyt = sig(S.activation(T.yt[:, :], T.y0[:, :], F.Identity, bias=T.colI[:, :]))
    sig(S.activation(T.win[:, 0:264], T.zb[:, 0:264], F.Identity, bias=T.colF[:, :]), fw)
    w("v", m_l2)
    tpb = sig(V.tensor_scalar(T.pb[:, :], ps[5][:, 0:64], -2047.5, None, A.add))
    tih = sig(V.tensor_scalar(T.ih[:, 0:128], cy(I4), 4.0, None, A.mult))
    w("v", tpb)
    tll = sig(V.tensor_tensor_scan(T.ll[:, 0:64], ps[5][:, 0:64], T.pb[:, :], 0.0, A.max, A.subtract))
    ttk = sig(V.tensor_scalar(T.tk[:, :], T.pb[:, :], XB + 65000.0, None, A.is_ge))

    def pick(q, win, lst, at_, u, v, out, tok, *toks):
        w(q, *toks)
        src, o = win.indirect(lst[:, at_ + u:at_ + v]), out[:, 16 * u:16 * v]
        sig(V.tensor_copy(o, src) if q == "v" else S.activation(o, src, F.Copy), tok)
    tng, tr1, tr2 = [new(), new()], new(), new()
    w("p", tcm, kq, k4)
    fold(ps[3][:, 0:64], T.cz, Z1, T.cm, False)
    w("p", tpb)
    m_lo = sig(mm(ps[3][:, 0:64], cy(IC), T.pb[:, :], False, True))
    pick("v", T.dat[:, 64:TW], T.ll, 0, 0, R1, T.r1, tr1, tll, tab1, zy)
    pick("s", T.dat[:, 64:TW], T.ll, 0, R1, 64, T.r1, tr1, tll, tab1, zy)
    w("p", ttk, ta)
    mm(ps[0][:, 0:64], cy(IM), T.tk[:, :], True, False)
    w("p", tr1)
    m_l3 = fold(ps[0][:, 0:64], T.cz, ZN, T.r1, first=False)
    w("v", m_lo)
    tll0 = sig(V.tensor_scalar(T.ll[:, 64:128], ps[3][:, 0:64], -XB / 16, 4095.0, A.add, A.min))
    sig(V.tensor_scalar(T.ih[:, 128:256], cy(I4), -4.0, None, A.mult), tih)
    pick("v", T.dat[:, 64:TW], T.ll, 64, 0, N1, T.ng, tng[0], tll0)
    pick("s", T.dat[:, 64:TW], T.ll, 64, N1, 64, T.ng, tng[1], tll0)
    w("v", m_l3)
    tl3 = sig(V.tensor_scalar(T.l3[:, :], ps[0][:, 0:64], 1.0 / 64, None, A.mult))
    pick("v", T.gat[:, :], T.l3, 0, 0, R2, T.r2, tr2, tl3, tab2)
    pick("s", T.gat[:, :], T.l3, 0, R2, 64, T.r2, tr2, tl3, tab2)
    w("p", twq)
    mm(ps[6][:, :], cz(FP), T.r1[:, 0:512], True, False)
    mm(ps[7][:, :], cz(FP), T.r1[:, 512:1024], True, False)
    w("p", tng[0], tng[1])
    m_ac = sig(mm(ps[6][:, :], cz(FN), T.ng[:, 0:512], False, True))
    m_ad = sig(mm(ps[7][:, :], cz(FN), T.ng[:, 512:1024], False, True))
    w("p", tr2)
    m_l4 = fold(ps[1][:, 0:64], T.cz, ZN, T.r2)
    tfd = [new(), new()]

    def sums(a, b):
        w("v", m_ac, m_ad, tr2)
        sig(V.tensor_tensor(T.fd[:, a:b], ps[6 + a // 512][:, a % 512:(b - 1) % 512 + 1], T.r2[:, a:b], A.add), tfd[a // 512])
    sums(0, 512)
    if FA > 512:
        sums(512, FA)

    w("v", m_l4)
    w("v", tyt)
    tl5 = sig(V.tensor_scalar(T.l5[:, :], ps[1][:, 0:64], 1.0 / 64, None, A.mult))
    f4 = sig(V.tensor_scalar(T.fl4[:, 8:72], ps[1][:, 0:64], 0.0, None, A.is_gt))
    sig(V.tensor_tensor(T.yb[:, 8:72], ps[1][:, 0:64], T.yt[:, :], A.min), f4)
    w("s", tl5)
    parts = ((0, PA), (PA, 64))
    tr3 = [sig(S.activation(T.r3[:, 16 * u:16 * v], T.dat[:, :].indirect(T.l5[:, u:v]), F.Copy)) for u, v in parts]
    sums(FA, FB)
    w("p", f4, zy, tol, fw, tih)
    mm(ps[2][:, 0:64], cy(FS), T.fl4[:, 7:71], True, False)
    mm(ps[2][:, 0:64], cy(FT), T.fl4[:, 8:72], False, False)
    mm(ps[2][:, 0:64], T.ih[:, 0:128], T.yb[:, 7:71], False, False)
    m_a = sig(mm(ps[2][:, 0:64], T.ih[:, 128:256], T.yb[:, 8:72], False, True))
    w("v", m_a)
    q5 = sig(V.tensor_tensor_scan(T.l4[:, :], ps[2][:, 0:64], T.c32[:, 0:64], T.colI[:, :], A.add, A.add))
    sums(FB, 1024)
    w("v", q5, fw)
    tw = new()
    for (u, v), t in zip(parts, tr3):
        w("v", tfd[0], tfd[(v - 1) // 32], t, tw)
        sig(V.tensor_tensor(T.win[:, :].indirect(T.l4[:, u:v]), T.fd[:, 16 * u:16 * v], T.r3[:, 16 * u:16 * v], A.add), tw)
    w("y", tw)
    t_y = new()
    w("s", tw)
    dsig(Y.dma_start(T.yk[:, :], T.win[RN:128:16, 1:257]), t_y)
    dsig(S.dma_start(T.ys[:, :], T.win[RS:128:16, 1:257]), t_y)
    for t in made:
        if waited.get(t[0], 0) < t[1]:
            w("y", t)
    g.wait_ge(T.sem.ls, ls[0])
